import numpy as np
import ml_dtypes


def mxq(x, axis, fmt="e4m3"):
    dtype, down = {"e4m3": (ml_dtypes.float8_e4m3fn, 7), "e5m2": (ml_dtypes.float8_e5m2, 14)}[fmt]
    v = np.moveaxis(np.asarray(x, np.float32).astype(ml_dtypes.bfloat16).astype(np.float64), axis, -1)
    blocks = v.reshape(v.shape[:-1] + (-1, 32))
    amax = np.abs(blocks).max(-1, keepdims=True)
    byte = np.maximum(np.where(amax > 0, np.frexp(amax)[1] - 1 + 127, 0) - down, 1)
    scale = np.exp2(byte - 127.0)
    codes = (blocks / scale).astype(np.float32).astype(dtype).astype(np.float64)
    return np.moveaxis((codes * scale).reshape(v.shape), -1, axis)


WIDE = False


def mx_kscale(k):
    if not WIDE:
        return np.ones(k)
    levels = np.array([10, -10, 5, -5, 0])
    if k % 512:
        return np.exp2(np.random.permutation(np.resize(levels, k // 32))).repeat(32)
    a = np.empty((k // 512, 16))
    for p in range(k // 512):
        a[p, :8] = np.random.permutation(np.resize(levels, 8))
        for g in range(8):
            far = levels[np.abs(levels - a[p, g]) >= 10]
            a[p, g + 8] = far[np.random.randint(len(far))]
    return np.exp2(a.ravel()).repeat(32)


def f64(x):
    return np.asarray(x).astype(np.float64)


def striped(idx):
    return np.tile(idx.reshape(-1, 16).T, (8, 1)).astype(np.uint16)


def unstriped(offs):
    return offs[:16].T.reshape(-1).astype(np.int64)


def pack_weight(w):
    k, n = w.shape
    w = f64(np.asarray(w, np.float32).astype(ml_dtypes.bfloat16)).reshape(k // 32, 32, n)
    amax = np.abs(w).max(1)
    byte = np.clip(np.where(amax > 0, np.frexp(amax)[1] - 1 + 127 - 7, 1), 1, 254)
    scaled = (w * np.exp2(127.0 - byte)[:, None, :]).reshape(k, n).astype(np.float32)
    words = np.ascontiguousarray(scaled.reshape(k // 512, 128, 4, n).transpose(0, 1, 3, 2)).astype(ml_dtypes.float8_e4m3fn).view(np.uint8)
    return words, np.ascontiguousarray(byte.astype(np.uint8).reshape(k // 512, 16, n))


def unpack_weight(words, scales):
    g, p, n, _ = words.shape
    vals = np.ascontiguousarray(words).view(ml_dtypes.float8_e4m3fn).astype(np.float64) * np.repeat(np.exp2(scales.astype(np.float64) - 127.0), 8, axis=1)[..., None]
    return vals.transpose(0, 1, 3, 2).reshape(g * 512, n)


K, T, S, H, N = 1024, 1024, 512, 512, 256


def setup_inputs():
    n = np.random.standard_normal
    s = mx_kscale(K)[:, None]
    u = mx_kscale(H)
    packed_xT = pack_weight(n((K, T)) * s)
    packed_w2 = pack_weight(n((H, N)) / np.sqrt(H) / u[:, None])
    return {
        "x_words": packed_xT[0],
        "x_scales": packed_xT[1],
        "w1": (n((K, H)) / np.sqrt(K) / s * u).astype(np.float32),
        "w2_words": packed_w2[0],
        "w2_scales": packed_w2[1],
        "pe": (0.5 * n((H, T)) * u[:, None]).astype(np.float32),
        "offs": striped(np.random.permutation(T)[:S]),
    }


def reference(x_words, x_scales, w1, w2_words, w2_scales, pe, offs):
    xq = unpack_weight(x_words, x_scales)[:, unstriped(offs)]
    g = f64(pe)[:, unstriped(offs)]
    h = (mxq(f64(w1), 0, "e4m3").T @ xq) + g
    return unpack_weight(w2_words, w2_scales).T @ mxq(h, 0, "e4m3")

@@ -1,0 +1,184 @@
+from contextlib import ExitStack
+
+import concourse.mybir as mybir
+
+K, T, S, H, N = 1024, 1024, 512, 512, 256
+FLOPS = 2 * K * H * S + 2 * H * N * S
+
+F32 = mybir.dt.float32
+BF16 = mybir.dt.bfloat16
+I32 = mybir.dt.int32
+U32 = mybir.dt.uint32
+U16 = mybir.dt.uint16
+U8 = mybir.dt.uint8
+FP8X4 = mybir.dt.float8_e4m3fn_x4
+ADD = mybir.AluOpType.add
+
+P = 128
+PACK = 4
+PASSES = K // (P * PACK)
+CHUNK = 128
+CHUNKS = S // CHUNK
+
+
+def tile_picked_posadd_none_p_kernel(
+    tc, x_words, x_scales, w1, w2_words, w2_scales, pe, offs, out
+):
+    nc = tc.nc
+    with ExitStack() as ctx:
+        keep = ctx.enter_context(tc.tile_pool(name="keep", bufs=1))
+        psum = ctx.enter_context(tc.psum_pool(name="psum", bufs=1))
+        offsets = keep.tile([P, S // 16], U16, name="offsets")
+        x_scale_rows = keep.tile([P, T], U8, name="x_scale_rows", align_bytes=64)
+        nc.vector.memset(x_scale_rows[:].bitcast(I32), 0)
+        w2_scale_rows = keep.tile([P, N], U8, name="w2_scale_rows", align_bytes=64)
+        nc.gpsimd.memset(w2_scale_rows[:].bitcast(I32), 0)
+        nc.scalar.dma_start(x_scale_rows[0 : 8, :].bitcast(I32), x_scales[:, 0 : 4, :].bitcast(I32))
+        nc.scalar.dma_start(x_scale_rows[32 : 40, :].bitcast(I32), x_scales[:, 4 : 8, :].bitcast(I32))
+        nc.scalar.dma_start(x_scale_rows[64 : 72, :].bitcast(I32), x_scales[:, 8 : 12, :].bitcast(I32))
+        nc.scalar.dma_start(x_scale_rows[96 : 104, :].bitcast(I32), x_scales[:, 12 : 16, :].bitcast(I32))
+        pe_rows = pe.rearrange("(p t) c -> p t c", t=PACK)
+        w1_rows = w1.rearrange("(z p j) c -> z p j c", p=P, j=PACK)
+        x_all0 = keep.tile([P, T], U32, name="x_all0", align_bytes=64)
+        nc.sync.dma_start(x_all0[:].bitcast(I32), x_words[0].rearrange("p n r -> p (n r)").bitcast(I32))
+        nc.sync.dma_start(offsets[:], offs)
+        x_all1 = keep.tile([P, T], U32, name="x_all1", align_bytes=64)
+        nc.sync.dma_start(x_all1[:].bitcast(I32), x_words[1].rearrange("p n r -> p (n r)").bitcast(I32))
+        pe_all0 = keep.tile([P, T], F32, name="pe_all0", align_bytes=64)
+        nc.sync.dma_start(pe_all0[:], pe_rows[:, 0, :])
+        raw_w0 = keep.tile([P, 4, H], F32, name="raw_w0", align_bytes=64)
+        nc.sync.dma_start(raw_w0[:], w1_rows[0, :, 0:4, :])
+        raw_w1a = keep.tile([P, 2, H], F32, name="raw_w1a", align_bytes=64)
+        nc.sync.dma_start(raw_w1a[:], w1_rows[1, :, 0:2, :])
+        raw_w1b = keep.tile([P, 2, H], F32, name="raw_w1b", align_bytes=64)
+        nc.sync.dma_start(raw_w1b[:], w1_rows[1, :, 2:4, :])
+        w2_codes = keep.tile([P, N], U32, name="w2_codes", align_bytes=64)
+        nc.sync.dma_start(w2_codes[:].bitcast(I32), w2_words[0].rearrange("p n r -> p (n r)").bitcast(I32))
+        pe_all1 = keep.tile([P, T], F32, name="pe_all1", align_bytes=64)
+        nc.sync.dma_start(pe_all1[:], pe_rows[:, 1, :])
+        pe_all2 = keep.tile([P, T], F32, name="pe_all2", align_bytes=64)
+        nc.sync.dma_start(pe_all2[:], pe_rows[:, 2, :])
+        pe_all3 = keep.tile([P, T], F32, name="pe_all3", align_bytes=64)
+        nc.sync.dma_start(pe_all3[:], pe_rows[:, 3, :])
+        nc.sync.dma_start(w2_scale_rows[0 : 4, :].bitcast(I32), w2_scales[0, 0 : 4, :].bitcast(I32))
+        nc.sync.dma_start(w2_scale_rows[32 : 36, :].bitcast(I32), w2_scales[0, 4 : 8, :].bitcast(I32))
+        nc.sync.dma_start(w2_scale_rows[64 : 68, :].bitcast(I32), w2_scales[0, 8 : 12, :].bitcast(I32))
+        nc.sync.dma_start(w2_scale_rows[96 : 100, :].bitcast(I32), w2_scales[0, 12 : 16, :].bitcast(I32))
+        picked = keep.tile([P, PACK, S], F32, name="picked", align_bytes=64)
+        x_planes = keep.tile([P, S], U8, name="x_planes", align_bytes=64)
+        x_codes0 = keep.tile([P, S], U32, name="x_codes0", align_bytes=64)
+        w1_grouped0 = keep.tile([P, PACK * H], BF16, name="w1_grouped0", align_bytes=64)
+        w1_codes0 = keep.tile([P, H], U32, name="w1_codes0", align_bytes=64)
+        w1_plane0 = keep.tile([P, H], U8, name="w1_plane0", align_bytes=64)
+        x_codes1 = keep.tile([P, S], U32, name="x_codes1", align_bytes=64)
+        w1_grouped1 = keep.tile([P, PACK * H], BF16, name="w1_grouped1", align_bytes=64)
+        w1_codes1 = keep.tile([P, H], U32, name="w1_codes1", align_bytes=64)
+        w1_plane1 = keep.tile([P, H], U8, name="w1_plane1", align_bytes=64)
+        nc.vector.tensor_copy(x_codes0[:], x_all0[:].indirect(offsets[:]))
+        nc.vector.tensor_copy(x_codes1[:], x_all1[:].indirect(offsets[:]))
+        nc.vector.tensor_copy(x_planes[:], x_scale_rows[:].indirect(offsets[:]))
+        nc.vector.tensor_copy(picked[:, 0, :], pe_all0[:].indirect(offsets[:]))
+        dst = w1_grouped0[:].rearrange("p (t m j) -> p m j t", t=PACK, j=PACK)[:, :, 0:4, :]
+        src = raw_w0[:].rearrange("p j (m t) -> p m j t", t=PACK)
+        nc.vector.tensor_copy(dst[:, :64], src[:, :64])
+        nc.scalar.copy(dst[:, 64:], src[:, 64:])
+        nc.vector.quantize_mx(out=w1_codes0[:].bitcast(FP8X4), scales=w1_plane0[:], in_=w1_grouped0[:])
+        dst = w1_grouped1[:].rearrange("p (t m j) -> p m j t", t=PACK, j=PACK)[:, :, 0:2, :]
+        src = raw_w1a[:].rearrange("p j (m t) -> p m j t", t=PACK)
+        nc.vector.tensor_copy(dst[:, :64], src[:, :64])
+        nc.scalar.copy(dst[:, 64:], src[:, 64:])
+        dst = w1_grouped1[:].rearrange("p (t m j) -> p m j t", t=PACK, j=PACK)[:, :, 2:4, :]
+        src = raw_w1b[:].rearrange("p j (m t) -> p m j t", t=PACK)
+        nc.vector.tensor_copy(dst[:, :84], src[:, :84])
+        nc.scalar.copy(dst[:, 84:], src[:, 84:])
+        nc.vector.quantize_mx(out=w1_codes1[:].bitcast(FP8X4), scales=w1_plane1[:], in_=w1_grouped1[:])
+        h_banks = []
+        for c in range(CHUNKS):
+            bank = psum.tile([P, PACK, CHUNK], F32, name=f"h_bank{c}")
+            cols = slice(c * CHUNK, (c + 1) * CHUNK)
+            for t in range(PACK):
+                rows = slice(t * P, (t + 1) * P)
+                for z, (wc, wp, xc) in enumerate(((w1_codes0, w1_plane0, x_codes0), (w1_codes1, w1_plane1, x_codes1))):
+                    nc.tensor.matmul_mx(
+                        out=bank[:, t, :],
+                        lhsT=wc[:, rows].bitcast(FP8X4),
+                        lhsT_scale=wp[:, rows],
+                        rhs=xc[:, cols].bitcast(FP8X4),
+                        rhs_scale=x_planes[4 * z : P, cols],
+                        start=(z == 0),
+                        stop=(z == PASSES - 1),
+                    )
+            h_banks.append(bank)
+        nc.vector.tensor_copy(picked[:, 1, :], pe_all1[:].indirect(offsets[:]))
+        nc.vector.tensor_copy(picked[:, 2, :], pe_all2[:].indirect(offsets[:]))
+        nc.vector.tensor_copy(picked[:, 3, 0:256], pe_all3[:].indirect(offsets[:, 0:16]))
+        nc.vector.tensor_copy(picked[:, 3, 256:512], pe_all3[:].indirect(offsets[:, 16:32]))
+        out_rows = out.rearrange("(b p) s -> p b s", p=P)
+        h_grouped0 = keep.tile([P, PACK * 128], BF16, name="h_grouped0", align_bytes=64)
+        nc.vector.tensor_tensor(
+            h_grouped0[:].rearrange("p (g i t) -> p g t i", i=4, t=PACK),
+            h_banks[0][:, :, 0:128].rearrange("p t (g i) -> p g t i", i=4),
+            picked[:, :, 0:128].rearrange("p t (g i) -> p g t i", i=4),
+            ADD,
+        )
+        h_grouped1 = keep.tile([P, PACK * 128], BF16, name="h_grouped1", align_bytes=64)
+        nc.vector.tensor_tensor(
+            h_grouped1[:].rearrange("p (g i t) -> p g t i", i=4, t=PACK),
+            h_banks[1][:, :, 0:128].rearrange("p t (g i) -> p g t i", i=4),
+            picked[:, :, 128:256].rearrange("p t (g i) -> p g t i", i=4),
+            ADD,
+        )
+        h_codes0 = keep.tile([P, 128], U32, name="h_codes0", align_bytes=64)
+        h_plane0 = keep.tile([P, 128], U8, name="h_plane0", align_bytes=64)
+        nc.vector.quantize_mx(out=h_codes0[:].bitcast(FP8X4), scales=h_plane0[:], in_=h_grouped0[:])
+        ob = psum.tile([P, 2, 128], F32, name="ob0", tag="out_bank0")
+        nc.tensor.matmul_mx(out=ob[:, 0, :], lhsT=w2_codes[:, 0:128].bitcast(FP8X4), lhsT_scale=w2_scale_rows[:, 0:128], rhs=h_codes0[:].bitcast(FP8X4), rhs_scale=h_plane0[:], start=True, stop=True)
+        nc.tensor.matmul_mx(out=ob[:, 1, :], lhsT=w2_codes[:, 128:256].bitcast(FP8X4), lhsT_scale=w2_scale_rows[:, 128:256], rhs=h_codes0[:].bitcast(FP8X4), rhs_scale=h_plane0[:], start=True, stop=True)
+        result0 = keep.tile([P, 2, 128], F32, name="result0", align_bytes=64)
+        nc.scalar.copy(result0[:], ob[:])
+        nc.sync.dma_start(out_rows[:, :, 0:128], result0[:])
+        h_grouped2 = keep.tile([P, PACK * 128], BF16, name="h_grouped2", align_bytes=64)
+        nc.vector.tensor_tensor(
+            h_grouped2[:].rearrange("p (g i t) -> p g t i", i=4, t=PACK),
+            h_banks[2][:, :, 0:128].rearrange("p t (g i) -> p g t i", i=4),
+            picked[:, :, 256:384].rearrange("p t (g i) -> p g t i", i=4),
+            ADD,
+        )
+        h_codes1 = keep.tile([P, 128], U32, name="h_codes1", align_bytes=64)
+        h_plane1 = keep.tile([P, 128], U8, name="h_plane1", align_bytes=64)
+        nc.vector.quantize_mx(out=h_codes1[:].bitcast(FP8X4), scales=h_plane1[:], in_=h_grouped1[:])
+        ob = psum.tile([P, 2, 128], F32, name="ob1", tag="out_bank1")
+        nc.tensor.matmul_mx(out=ob[:, 0, :], lhsT=w2_codes[:, 0:128].bitcast(FP8X4), lhsT_scale=w2_scale_rows[:, 0:128], rhs=h_codes1[:].bitcast(FP8X4), rhs_scale=h_plane1[:], start=True, stop=True)
+        nc.tensor.matmul_mx(out=ob[:, 1, :], lhsT=w2_codes[:, 128:256].bitcast(FP8X4), lhsT_scale=w2_scale_rows[:, 128:256], rhs=h_codes1[:].bitcast(FP8X4), rhs_scale=h_plane1[:], start=True, stop=True)
+        result1 = keep.tile([P, 2, 128], F32, name="result1", align_bytes=64)
+        nc.scalar.copy(result1[:], ob[:])
+        nc.sync.dma_start(out_rows[:, :, 128:256], result1[:])
+        h_grouped3 = keep.tile([P, PACK * 128], BF16, name="h_grouped3", align_bytes=64)
+        nc.vector.tensor_tensor(
+            h_grouped3[:].rearrange("p (g i t) -> p g t i", i=4, t=PACK),
+            h_banks[3][:, :, 0:128].rearrange("p t (g i) -> p g t i", i=4),
+            picked[:, :, 384:512].rearrange("p t (g i) -> p g t i", i=4),
+            ADD,
+        )
+        h_codes2 = keep.tile([P, 128], U32, name="h_codes2", align_bytes=64)
+        h_plane2 = keep.tile([P, 128], U8, name="h_plane2", align_bytes=64)
+        nc.vector.quantize_mx(out=h_codes2[:].bitcast(FP8X4), scales=h_plane2[:], in_=h_grouped2[:])
+        ob = psum.tile([P, 2, 128], F32, name="ob2", tag="h_bank0")
+        nc.tensor.matmul_mx(out=ob[:, 0, :], lhsT=w2_codes[:, 0:128].bitcast(FP8X4), lhsT_scale=w2_scale_rows[:, 0:128], rhs=h_codes2[:].bitcast(FP8X4), rhs_scale=h_plane2[:], start=True, stop=True)
+        nc.tensor.matmul_mx(out=ob[:, 1, :], lhsT=w2_codes[:, 128:256].bitcast(FP8X4), lhsT_scale=w2_scale_rows[:, 128:256], rhs=h_codes2[:].bitcast(FP8X4), rhs_scale=h_plane2[:], start=True, stop=True)
+        result2 = keep.tile([P, 2, 128], F32, name="result2", align_bytes=64)
+        nc.scalar.copy(result2[:], ob[:])
+        nc.sync.dma_start(out_rows[:, :, 256:384], result2[:])
+        h_codes3 = keep.tile([P, 128], U32, name="h_codes3", align_bytes=64)
+        h_plane3 = keep.tile([P, 128], U8, name="h_plane3", align_bytes=64)
+        nc.vector.quantize_mx(out=h_codes3[:].bitcast(FP8X4), scales=h_plane3[:], in_=h_grouped3[:])
+        ob = psum.tile([P, 128], F32, name="obl0", tag="out_last0")
+        nc.tensor.matmul_mx(out=ob[:], lhsT=w2_codes[:, 0:128].bitcast(FP8X4), lhsT_scale=w2_scale_rows[:, 0:128], rhs=h_codes3[:].bitcast(FP8X4), rhs_scale=h_plane3[:], start=True, stop=True)
+        resl0 = keep.tile([P, 128], F32, name="resl0", align_bytes=64)
+        nc.scalar.copy(resl0[:], ob[:])
+        nc.scalar.dma_start(out_rows[:, 0, 384:512], resl0[:])
+        ob = psum.tile([P, 128], F32, name="obl1", tag="out_last1")
+        nc.tensor.matmul_mx(out=ob[:], lhsT=w2_codes[:, 128:256].bitcast(FP8X4), lhsT_scale=w2_scale_rows[:, 128:256], rhs=h_codes3[:].bitcast(FP8X4), rhs_scale=h_plane3[:], start=True, stop=True)
+        resl1 = keep.tile([P, 128], F32, name="resl1", align_bytes=64)
+        nc.vector.tensor_copy(resl1[:], ob[:])
+        nc.sync.dma_start(out_rows[:, 1, 384:512], resl1[:])

@@ -116,16 +116,16 @@ def tile_picked_posadd_none_p_kernel(
         out_rows = out.rearrange("(b p) s -> p b s", p=P)
         h_grouped0 = keep.tile([P, PACK * 128], BF16, name="h_grouped0", align_bytes=64)
         nc.vector.tensor_tensor(
-            h_grouped0[:].rearrange("p (g i t) -> p g t i", i=4, t=PACK),
-            h_banks[0][:, :, 0:128].rearrange("p t (g i) -> p g t i", i=4),
-            picked[:, :, 0:128].rearrange("p t (g i) -> p g t i", i=4),
+            h_grouped0[:].rearrange("p (g i t) -> p g t i", i=2, t=PACK),
+            h_banks[0][:, :, 0:128].rearrange("p t (g i) -> p g t i", i=2),
+            picked[:, :, 0:128].rearrange("p t (g i) -> p g t i", i=2),
             ADD,
         )
         h_grouped1 = keep.tile([P, PACK * 128], BF16, name="h_grouped1", align_bytes=64)
         nc.vector.tensor_tensor(
-            h_grouped1[:].rearrange("p (g i t) -> p g t i", i=4, t=PACK),
-            h_banks[1][:, :, 0:128].rearrange("p t (g i) -> p g t i", i=4),
-            picked[:, :, 128:256].rearrange("p t (g i) -> p g t i", i=4),
+            h_grouped1[:].rearrange("p (g i t) -> p g t i", i=2, t=PACK),
+            h_banks[1][:, :, 0:128].rearrange("p t (g i) -> p g t i", i=2),
+            picked[:, :, 128:256].rearrange("p t (g i) -> p g t i", i=2),
             ADD,
         )
         h_codes0 = keep.tile([P, 128], U32, name="h_codes0", align_bytes=64)
@@ -139,9 +139,9 @@ def tile_picked_posadd_none_p_kernel(
         nc.sync.dma_start(out_rows[:, :, 0:128], result0[:])
         h_grouped2 = keep.tile([P, PACK * 128], BF16, name="h_grouped2", align_bytes=64)
         nc.vector.tensor_tensor(
-            h_grouped2[:].rearrange("p (g i t) -> p g t i", i=4, t=PACK),
-            h_banks[2][:, :, 0:128].rearrange("p t (g i) -> p g t i", i=4),
-            picked[:, :, 256:384].rearrange("p t (g i) -> p g t i", i=4),
+            h_grouped2[:].rearrange("p (g i t) -> p g t i", i=2, t=PACK),
+            h_banks[2][:, :, 0:128].rearrange("p t (g i) -> p g t i", i=2),
+            picked[:, :, 256:384].rearrange("p t (g i) -> p g t i", i=2),
             ADD,
         )
         h_codes1 = keep.tile([P, 128], U32, name="h_codes1", align_bytes=64)
@@ -155,9 +155,9 @@ def tile_picked_posadd_none_p_kernel(
         nc.sync.dma_start(out_rows[:, :, 128:256], result1[:])
         h_grouped3 = keep.tile([P, PACK * 128], BF16, name="h_grouped3", align_bytes=64)
         nc.vector.tensor_tensor(
-            h_grouped3[:].rearrange("p (g i t) -> p g t i", i=4, t=PACK),
-            h_banks[3][:, :, 0:128].rearrange("p t (g i) -> p g t i", i=4),
-            picked[:, :, 384:512].rearrange("p t (g i) -> p g t i", i=4),
+            h_grouped3[:].rearrange("p (g i t) -> p g t i", i=2, t=PACK),
+            h_banks[3][:, :, 0:128].rearrange("p t (g i) -> p g t i", i=2),
+            picked[:, :, 384:512].rearrange("p t (g i) -> p g t i", i=2),
             ADD,
         )
         h_codes2 = keep.tile([P, 128], U32, name="h_codes2", align_bytes=64)

@@ -33,21 +33,21 @@ def tile_picked_posadd_none_p_kernel(
         nc.vector.memset(x_scale_rows[:].bitcast(I32), 0)
         w2_scale_rows = keep.tile([P, N], U8, name="w2_scale_rows", align_bytes=64)
         nc.gpsimd.memset(w2_scale_rows[:].bitcast(I32), 0)
-        nc.scalar.dma_start(x_scale_rows[0 : 8, :].bitcast(I32), x_scales[:, 0 : 4, :].bitcast(I32))
-        nc.scalar.dma_start(x_scale_rows[32 : 40, :].bitcast(I32), x_scales[:, 4 : 8, :].bitcast(I32))
-        nc.scalar.dma_start(x_scale_rows[64 : 72, :].bitcast(I32), x_scales[:, 8 : 12, :].bitcast(I32))
-        nc.scalar.dma_start(x_scale_rows[96 : 104, :].bitcast(I32), x_scales[:, 12 : 16, :].bitcast(I32))
         pe_rows = pe.rearrange("(p t) c -> p t c", t=PACK)
         w1_rows = w1.rearrange("(z p j) c -> z p j c", p=P, j=PACK)
         x_all0 = keep.tile([P, T], U32, name="x_all0", align_bytes=64)
         nc.sync.dma_start(x_all0[:].bitcast(I32), x_words[0].rearrange("p n r -> p (n r)").bitcast(I32))
         nc.sync.dma_start(offsets[:], offs)
+        nc.sync.dma_start(x_scale_rows[0 : 8, :].bitcast(I32), x_scales[:, 0 : 4, :].bitcast(I32))
+        nc.sync.dma_start(x_scale_rows[32 : 40, :].bitcast(I32), x_scales[:, 4 : 8, :].bitcast(I32))
+        nc.sync.dma_start(x_scale_rows[64 : 72, :].bitcast(I32), x_scales[:, 8 : 12, :].bitcast(I32))
+        nc.sync.dma_start(x_scale_rows[96 : 104, :].bitcast(I32), x_scales[:, 12 : 16, :].bitcast(I32))
+        raw_w0 = keep.tile([P, 4, H], F32, name="raw_w0", align_bytes=64)
+        nc.sync.dma_start(raw_w0[:], w1_rows[0, :, 0:4, :])
         x_all1 = keep.tile([P, T], U32, name="x_all1", align_bytes=64)
         nc.sync.dma_start(x_all1[:].bitcast(I32), x_words[1].rearrange("p n r -> p (n r)").bitcast(I32))
         pe_all0 = keep.tile([P, T], F32, name="pe_all0", align_bytes=64)
         nc.sync.dma_start(pe_all0[:], pe_rows[:, 0, :])
-        raw_w0 = keep.tile([P, 4, H], F32, name="raw_w0", align_bytes=64)
-        nc.sync.dma_start(raw_w0[:], w1_rows[0, :, 0:4, :])
         raw_w1a = keep.tile([P, 2, H], F32, name="raw_w1a", align_bytes=64)
         nc.sync.dma_start(raw_w1a[:], w1_rows[1, :, 0:2, :])
         raw_w1b = keep.tile([P, 2, H], F32, name="raw_w1b", align_bytes=64)
@@ -75,22 +75,22 @@ def tile_picked_posadd_none_p_kernel(
         w1_codes1 = keep.tile([P, H], U32, name="w1_codes1", align_bytes=64)
         w1_plane1 = keep.tile([P, H], U8, name="w1_plane1", align_bytes=64)
         nc.vector.tensor_copy(x_codes0[:], x_all0[:].indirect(offsets[:]))
-        nc.vector.tensor_copy(x_codes1[:], x_all1[:].indirect(offsets[:]))
         nc.vector.tensor_copy(x_planes[:], x_scale_rows[:].indirect(offsets[:]))
-        nc.vector.tensor_copy(picked[:, 0, :], pe_all0[:].indirect(offsets[:]))
         dst = w1_grouped0[:].rearrange("p (t m j) -> p m j t", t=PACK, j=PACK)[:, :, 0:4, :]
         src = raw_w0[:].rearrange("p j (m t) -> p m j t", t=PACK)
-        nc.vector.tensor_copy(dst[:, :64], src[:, :64])
-        nc.scalar.copy(dst[:, 64:], src[:, 64:])
+        nc.vector.tensor_copy(dst[:, :, :, :2], src[:, :, :, :2])
+        nc.scalar.copy(dst[:, :, :, 2:], src[:, :, :, 2:])
         nc.vector.quantize_mx(out=w1_codes0[:].bitcast(FP8X4), scales=w1_plane0[:], in_=w1_grouped0[:])
+        nc.vector.tensor_copy(x_codes1[:], x_all1[:].indirect(offsets[:]))
+        nc.vector.tensor_copy(picked[:, 0, :], pe_all0[:].indirect(offsets[:]))
         dst = w1_grouped1[:].rearrange("p (t m j) -> p m j t", t=PACK, j=PACK)[:, :, 0:2, :]
         src = raw_w1a[:].rearrange("p j (m t) -> p m j t", t=PACK)
-        nc.vector.tensor_copy(dst[:, :64], src[:, :64])
-        nc.scalar.copy(dst[:, 64:], src[:, 64:])
+        nc.vector.tensor_copy(dst[:, :, :, :2], src[:, :, :, :2])
+        nc.scalar.copy(dst[:, :, :, 2:], src[:, :, :, 2:])
         dst = w1_grouped1[:].rearrange("p (t m j) -> p m j t", t=PACK, j=PACK)[:, :, 2:4, :]
         src = raw_w1b[:].rearrange("p j (m t) -> p m j t", t=PACK)
-        nc.vector.tensor_copy(dst[:, :84], src[:, :84])
-        nc.scalar.copy(dst[:, 84:], src[:, 84:])
+        nc.vector.tensor_copy(dst[:, :, :, :3], src[:, :, :, :3])
+        nc.scalar.copy(dst[:, :, :, 3:], src[:, :, :, 3:])
         nc.vector.quantize_mx(out=w1_codes1[:].bitcast(FP8X4), scales=w1_plane1[:], in_=w1_grouped1[:])
         h_banks = []
         for c in range(CHUNKS):

@@ -42,24 +42,26 @@ def tile_picked_posadd_none_p_kernel(
         nc.sync.dma_start(x_scale_rows[32 : 40, :].bitcast(I32), x_scales[:, 4 : 8, :].bitcast(I32))
         nc.sync.dma_start(x_scale_rows[64 : 72, :].bitcast(I32), x_scales[:, 8 : 12, :].bitcast(I32))
         nc.sync.dma_start(x_scale_rows[96 : 104, :].bitcast(I32), x_scales[:, 12 : 16, :].bitcast(I32))
-        raw_w0 = keep.tile([P, 4, H], F32, name="raw_w0", align_bytes=64)
-        nc.sync.dma_start(raw_w0[:], w1_rows[0, :, 0:4, :])
         x_all1 = keep.tile([P, T], U32, name="x_all1", align_bytes=64)
         nc.sync.dma_start(x_all1[:].bitcast(I32), x_words[1].rearrange("p n r -> p (n r)").bitcast(I32))
-        pe_all0 = keep.tile([P, T], F32, name="pe_all0", align_bytes=64)
-        nc.sync.dma_start(pe_all0[:], pe_rows[:, 0, :])
+        raw_w0a = keep.tile([P, 2, H], F32, name="raw_w0a", align_bytes=64)
+        nc.sync.dma_start(raw_w0a[:], w1_rows[0, :, 0:2, :])
+        raw_w0b = keep.tile([P, 2, H], F32, name="raw_w0b", align_bytes=64)
+        nc.sync.dma_start(raw_w0b[:], w1_rows[0, :, 2:4, :])
         raw_w1a = keep.tile([P, 2, H], F32, name="raw_w1a", align_bytes=64)
         nc.sync.dma_start(raw_w1a[:], w1_rows[1, :, 0:2, :])
+        pe_all0 = keep.tile([P, T], F32, name="pe_all0", align_bytes=64)
+        nc.sync.dma_start(pe_all0[:], pe_rows[:, 0, :])
         raw_w1b = keep.tile([P, 2, H], F32, name="raw_w1b", align_bytes=64)
         nc.sync.dma_start(raw_w1b[:], w1_rows[1, :, 2:4, :])
-        w2_codes = keep.tile([P, N], U32, name="w2_codes", align_bytes=64)
-        nc.sync.dma_start(w2_codes[:].bitcast(I32), w2_words[0].rearrange("p n r -> p (n r)").bitcast(I32))
         pe_all1 = keep.tile([P, T], F32, name="pe_all1", align_bytes=64)
         nc.sync.dma_start(pe_all1[:], pe_rows[:, 1, :])
         pe_all2 = keep.tile([P, T], F32, name="pe_all2", align_bytes=64)
         nc.sync.dma_start(pe_all2[:], pe_rows[:, 2, :])
         pe_all3 = keep.tile([P, T], F32, name="pe_all3", align_bytes=64)
         nc.sync.dma_start(pe_all3[:], pe_rows[:, 3, :])
+        w2_codes = keep.tile([P, N], U32, name="w2_codes", align_bytes=64)
+        nc.sync.dma_start(w2_codes[:].bitcast(I32), w2_words[0].rearrange("p n r -> p (n r)").bitcast(I32))
         nc.sync.dma_start(w2_scale_rows[0 : 4, :].bitcast(I32), w2_scales[0, 0 : 4, :].bitcast(I32))
         nc.sync.dma_start(w2_scale_rows[32 : 36, :].bitcast(I32), w2_scales[0, 4 : 8, :].bitcast(I32))
         nc.sync.dma_start(w2_scale_rows[64 : 68, :].bitcast(I32), w2_scales[0, 8 : 12, :].bitcast(I32))
@@ -76,22 +78,28 @@ def tile_picked_posadd_none_p_kernel(
         w1_plane1 = keep.tile([P, H], U8, name="w1_plane1", align_bytes=64)
         nc.vector.tensor_copy(x_codes0[:], x_all0[:].indirect(offsets[:]))
         nc.vector.tensor_copy(x_planes[:], x_scale_rows[:].indirect(offsets[:]))
-        dst = w1_grouped0[:].rearrange("p (t m j) -> p m j t", t=PACK, j=PACK)[:, :, 0:4, :]
-        src = raw_w0[:].rearrange("p j (m t) -> p m j t", t=PACK)
+        nc.vector.tensor_copy(x_codes1[:], x_all1[:].indirect(offsets[:]))
+        dst = w1_grouped0[:].rearrange("p (t m j) -> p m j t", t=PACK, j=PACK)[:, :, 0:2, :]
+        src = raw_w0a[:].rearrange("p j (m t) -> p m j t", t=PACK)
+        nc.vector.tensor_copy(dst[:, :, :, :2], src[:, :, :, :2])
+        nc.scalar.copy(dst[:, :, :, 2:], src[:, :, :, 2:])
+        dst = w1_grouped0[:].rearrange("p (t m j) -> p m j t", t=PACK, j=PACK)[:, :, 2:4, :]
+        src = raw_w0b[:].rearrange("p j (m t) -> p m j t", t=PACK)
         nc.vector.tensor_copy(dst[:, :, :, :2], src[:, :, :, :2])
         nc.scalar.copy(dst[:, :, :, 2:], src[:, :, :, 2:])
         nc.vector.quantize_mx(out=w1_codes0[:].bitcast(FP8X4), scales=w1_plane0[:], in_=w1_grouped0[:])
-        nc.vector.tensor_copy(x_codes1[:], x_all1[:].indirect(offsets[:]))
-        nc.vector.tensor_copy(picked[:, 0, :], pe_all0[:].indirect(offsets[:]))
         dst = w1_grouped1[:].rearrange("p (t m j) -> p m j t", t=PACK, j=PACK)[:, :, 0:2, :]
         src = raw_w1a[:].rearrange("p j (m t) -> p m j t", t=PACK)
         nc.vector.tensor_copy(dst[:, :, :, :2], src[:, :, :, :2])
         nc.scalar.copy(dst[:, :, :, 2:], src[:, :, :, 2:])
+        nc.vector.tensor_copy(picked[:, 0, :], pe_all0[:].indirect(offsets[:]))
         dst = w1_grouped1[:].rearrange("p (t m j) -> p m j t", t=PACK, j=PACK)[:, :, 2:4, :]
         src = raw_w1b[:].rearrange("p j (m t) -> p m j t", t=PACK)
-        nc.vector.tensor_copy(dst[:, :, :, :3], src[:, :, :, :3])
+        nc.vector.tensor_copy(dst[:, :, :, :2], src[:, :, :, :2])
+        nc.vector.tensor_copy(dst[:, :, :, 2:3], src[:, :, :, 2:3])
         nc.scalar.copy(dst[:, :, :, 3:], src[:, :, :, 3:])
-        nc.vector.quantize_mx(out=w1_codes1[:].bitcast(FP8X4), scales=w1_plane1[:], in_=w1_grouped1[:])
+        nc.vector.quantize_mx(out=w1_codes1[:, 0:256].bitcast(FP8X4), scales=w1_plane1[:, 0:256], in_=w1_grouped1[:, 0:1024])
+        nc.vector.quantize_mx(out=w1_codes1[:, 256:512].bitcast(FP8X4), scales=w1_plane1[:, 256:512], in_=w1_grouped1[:, 1024:2048])
         h_banks = []
         for c in range(CHUNKS):
             bank = psum.tile([P, PACK, CHUNK], F32, name=f"h_bank{c}")

@@ -17,8 +17,10 @@ ADD = mybir.AluOpType.add
 P = 128
 PACK = 4
 PASSES = K // (P * PACK)
+HALF = S // 2
 CHUNK = 128
 CHUNKS = S // CHUNK
+LIST_ROWS = 16
 
 
 def tile_picked_posadd_none_p_kernel(
@@ -28,165 +30,166 @@ def tile_picked_posadd_none_p_kernel(
     with ExitStack() as ctx:
         keep = ctx.enter_context(tc.tile_pool(name="keep", bufs=1))
         psum = ctx.enter_context(tc.psum_pool(name="psum", bufs=1))
-        offsets = keep.tile([P, S // 16], U16, name="offsets")
-        x_scale_rows = keep.tile([P, T], U8, name="x_scale_rows", align_bytes=64)
+
+        def sbuf(name, shape, dtype, tag=None):
+            return keep.tile(shape, dtype, name=name, tag=tag or name, align_bytes=64)
+
+        def entries(first, count):
+            return offsets[:, first // LIST_ROWS : (first + count) // LIST_ROWS]
+
+        offsets = keep.tile([P, S // LIST_ROWS], U16, name="offsets")
+        x_scale_rows = sbuf("x_scale_rows", [P, T], U8)
         nc.vector.memset(x_scale_rows[:].bitcast(I32), 0)
-        w2_scale_rows = keep.tile([P, N], U8, name="w2_scale_rows", align_bytes=64)
+        w2_scale_rows = sbuf("w2_scale_rows", [P, N], U8)
         nc.gpsimd.memset(w2_scale_rows[:].bitcast(I32), 0)
+
         pe_rows = pe.rearrange("(p t) c -> p t c", t=PACK)
         w1_rows = w1.rearrange("(z p j) c -> z p j c", p=P, j=PACK)
-        x_all0 = keep.tile([P, T], U32, name="x_all0", align_bytes=64)
-        nc.sync.dma_start(x_all0[:].bitcast(I32), x_words[0].rearrange("p n r -> p (n r)").bitcast(I32))
+        x_all = [sbuf(f"x_all{z}", [P, T], U32) for z in range(PASSES)]
+        pieces = [(0, 0, 2, 32), (0, 2, 4, 80), (1, 0, 2, 0), (1, 2, 4, 104)]
+        w1_raw = [sbuf(f"w1_raw{i}", [P, j1 - j0, H], F32) for i, (z, j0, j1, cut) in enumerate(pieces)]
+        pe_all = [sbuf(f"pe_all{t}", [P, T], F32) for t in range(PACK)]
+        w2_codes = sbuf("w2_codes", [P, N], U32)
+
+        def load_words(tile, words):
+            nc.sync.dma_start(tile[:].bitcast(I32), words.rearrange("p n r -> p (n r)").bitcast(I32))
+
+        load_words(x_all[0], x_words[0])
         nc.sync.dma_start(offsets[:], offs)
-        nc.sync.dma_start(x_scale_rows[0 : 8, :].bitcast(I32), x_scales[:, 0 : 4, :].bitcast(I32))
-        nc.sync.dma_start(x_scale_rows[32 : 40, :].bitcast(I32), x_scales[:, 4 : 8, :].bitcast(I32))
-        nc.sync.dma_start(x_scale_rows[64 : 72, :].bitcast(I32), x_scales[:, 8 : 12, :].bitcast(I32))
-        nc.sync.dma_start(x_scale_rows[96 : 104, :].bitcast(I32), x_scales[:, 12 : 16, :].bitcast(I32))
-        x_all1 = keep.tile([P, T], U32, name="x_all1", align_bytes=64)
-        nc.sync.dma_start(x_all1[:].bitcast(I32), x_words[1].rearrange("p n r -> p (n r)").bitcast(I32))
-        raw_w0a = keep.tile([P, 2, H], F32, name="raw_w0a", align_bytes=64)
-        nc.sync.dma_start(raw_w0a[:], w1_rows[0, :, 0:2, :])
-        raw_w0b = keep.tile([P, 2, H], F32, name="raw_w0b", align_bytes=64)
-        nc.sync.dma_start(raw_w0b[:], w1_rows[0, :, 2:4, :])
-        raw_w1a = keep.tile([P, 2, H], F32, name="raw_w1a", align_bytes=64)
-        nc.sync.dma_start(raw_w1a[:], w1_rows[1, :, 0:2, :])
-        pe_all0 = keep.tile([P, T], F32, name="pe_all0", align_bytes=64)
-        nc.sync.dma_start(pe_all0[:], pe_rows[:, 0, :])
-        raw_w1b = keep.tile([P, 2, H], F32, name="raw_w1b", align_bytes=64)
-        nc.sync.dma_start(raw_w1b[:], w1_rows[1, :, 2:4, :])
-        pe_all1 = keep.tile([P, T], F32, name="pe_all1", align_bytes=64)
-        nc.sync.dma_start(pe_all1[:], pe_rows[:, 1, :])
-        pe_all2 = keep.tile([P, T], F32, name="pe_all2", align_bytes=64)
-        nc.sync.dma_start(pe_all2[:], pe_rows[:, 2, :])
-        pe_all3 = keep.tile([P, T], F32, name="pe_all3", align_bytes=64)
-        nc.sync.dma_start(pe_all3[:], pe_rows[:, 3, :])
-        w2_codes = keep.tile([P, N], U32, name="w2_codes", align_bytes=64)
-        nc.sync.dma_start(w2_codes[:].bitcast(I32), w2_words[0].rearrange("p n r -> p (n r)").bitcast(I32))
-        nc.sync.dma_start(w2_scale_rows[0 : 4, :].bitcast(I32), w2_scales[0, 0 : 4, :].bitcast(I32))
-        nc.sync.dma_start(w2_scale_rows[32 : 36, :].bitcast(I32), w2_scales[0, 4 : 8, :].bitcast(I32))
-        nc.sync.dma_start(w2_scale_rows[64 : 68, :].bitcast(I32), w2_scales[0, 8 : 12, :].bitcast(I32))
-        nc.sync.dma_start(w2_scale_rows[96 : 100, :].bitcast(I32), w2_scales[0, 12 : 16, :].bitcast(I32))
-        picked = keep.tile([P, PACK, S], F32, name="picked", align_bytes=64)
-        x_planes = keep.tile([P, S], U8, name="x_planes", align_bytes=64)
-        x_codes0 = keep.tile([P, S], U32, name="x_codes0", align_bytes=64)
-        w1_grouped0 = keep.tile([P, PACK * H], BF16, name="w1_grouped0", align_bytes=64)
-        w1_codes0 = keep.tile([P, H], U32, name="w1_codes0", align_bytes=64)
-        w1_plane0 = keep.tile([P, H], U8, name="w1_plane0", align_bytes=64)
-        x_codes1 = keep.tile([P, S], U32, name="x_codes1", align_bytes=64)
-        w1_grouped1 = keep.tile([P, PACK * H], BF16, name="w1_grouped1", align_bytes=64)
-        w1_codes1 = keep.tile([P, H], U32, name="w1_codes1", align_bytes=64)
-        w1_plane1 = keep.tile([P, H], U8, name="w1_plane1", align_bytes=64)
-        nc.vector.tensor_copy(x_codes0[:], x_all0[:].indirect(offsets[:]))
+        for q in range(4):
+            nc.sync.dma_start(
+                x_scale_rows[32 * q : 32 * q + 8, :].bitcast(I32), x_scales[:, 4 * q : 4 * q + 4, :].bitcast(I32)
+            )
+        for raw, (z, j0, j1, cut) in zip(w1_raw, pieces):
+            nc.sync.dma_start(raw[:], w1_rows[z, :, j0:j1, :])
+        load_words(x_all[1], x_words[1])
+        for t in range(PACK):
+            nc.sync.dma_start(pe_all[t][:], pe_rows[:, t, :])
+        load_words(w2_codes, w2_words[0])
+        for q in range(4):
+            nc.sync.dma_start(
+                w2_scale_rows[32 * q : 32 * q + 4, :].bitcast(I32), w2_scales[0, 4 * q : 4 * q + 4, :].bitcast(I32)
+            )
+
+        x_planes = sbuf("x_planes", [P, S], U8)
+        x_codes0 = sbuf("x_codes0", [P, S], U32)
+        x_codes1 = [sbuf(f"x_codes1{h}", [P, HALF], U32) for h in range(2)]
+        nc.vector.tensor_copy(x_codes0[:], x_all[0][:].indirect(offsets[:]))
         nc.vector.tensor_copy(x_planes[:], x_scale_rows[:].indirect(offsets[:]))
-        nc.vector.tensor_copy(x_codes1[:], x_all1[:].indirect(offsets[:]))
-        dst = w1_grouped0[:].rearrange("p (t m j) -> p m j t", t=PACK, j=PACK)[:, :, 0:2, :]
-        src = raw_w0a[:].rearrange("p j (m t) -> p m j t", t=PACK)
-        nc.vector.tensor_copy(dst[:, :, :, :2], src[:, :, :, :2])
-        nc.scalar.copy(dst[:, :, :, 2:], src[:, :, :, 2:])
-        dst = w1_grouped0[:].rearrange("p (t m j) -> p m j t", t=PACK, j=PACK)[:, :, 2:4, :]
-        src = raw_w0b[:].rearrange("p j (m t) -> p m j t", t=PACK)
-        nc.vector.tensor_copy(dst[:, :, :, :2], src[:, :, :, :2])
-        nc.scalar.copy(dst[:, :, :, 2:], src[:, :, :, 2:])
-        nc.vector.quantize_mx(out=w1_codes0[:].bitcast(FP8X4), scales=w1_plane0[:], in_=w1_grouped0[:])
-        dst = w1_grouped1[:].rearrange("p (t m j) -> p m j t", t=PACK, j=PACK)[:, :, 0:2, :]
-        src = raw_w1a[:].rearrange("p j (m t) -> p m j t", t=PACK)
-        nc.vector.tensor_copy(dst[:, :, :, :2], src[:, :, :, :2])
-        nc.scalar.copy(dst[:, :, :, 2:], src[:, :, :, 2:])
-        nc.vector.tensor_copy(picked[:, 0, :], pe_all0[:].indirect(offsets[:]))
-        dst = w1_grouped1[:].rearrange("p (t m j) -> p m j t", t=PACK, j=PACK)[:, :, 2:4, :]
-        src = raw_w1b[:].rearrange("p j (m t) -> p m j t", t=PACK)
-        nc.vector.tensor_copy(dst[:, :, :, :2], src[:, :, :, :2])
-        nc.vector.tensor_copy(dst[:, :, :, 2:3], src[:, :, :, 2:3])
-        nc.scalar.copy(dst[:, :, :, 3:], src[:, :, :, 3:])
-        nc.vector.quantize_mx(out=w1_codes1[:, 0:256].bitcast(FP8X4), scales=w1_plane1[:, 0:256], in_=w1_grouped1[:, 0:1024])
-        nc.vector.quantize_mx(out=w1_codes1[:, 256:512].bitcast(FP8X4), scales=w1_plane1[:, 256:512], in_=w1_grouped1[:, 1024:2048])
-        h_banks = []
-        for c in range(CHUNKS):
-            bank = psum.tile([P, PACK, CHUNK], F32, name=f"h_bank{c}")
-            cols = slice(c * CHUNK, (c + 1) * CHUNK)
-            for t in range(PACK):
-                rows = slice(t * P, (t + 1) * P)
-                for z, (wc, wp, xc) in enumerate(((w1_codes0, w1_plane0, x_codes0), (w1_codes1, w1_plane1, x_codes1))):
-                    nc.tensor.matmul_mx(
-                        out=bank[:, t, :],
-                        lhsT=wc[:, rows].bitcast(FP8X4),
-                        lhsT_scale=wp[:, rows],
-                        rhs=xc[:, cols].bitcast(FP8X4),
-                        rhs_scale=x_planes[4 * z : P, cols],
-                        start=(z == 0),
-                        stop=(z == PASSES - 1),
-                    )
-            h_banks.append(bank)
-        nc.vector.tensor_copy(picked[:, 1, :], pe_all1[:].indirect(offsets[:]))
-        nc.vector.tensor_copy(picked[:, 2, :], pe_all2[:].indirect(offsets[:]))
-        nc.vector.tensor_copy(picked[:, 3, 0:256], pe_all3[:].indirect(offsets[:, 0:16]))
-        nc.vector.tensor_copy(picked[:, 3, 256:512], pe_all3[:].indirect(offsets[:, 16:32]))
+
+        w1_codes, w1_planes = [], []
+        for z in range(PASSES):
+            grouped = sbuf(f"w1_grouped{z}", [P, PACK * H], BF16)
+            for raw, (piece_z, j0, j1, cut) in zip(w1_raw, pieces):
+                if piece_z == z:
+                    dst = grouped[:].rearrange("p (t m j) -> p m t j", t=PACK, j=PACK)[:, :, :, j0:j1]
+                    src = raw[:].rearrange("p j (m t) -> p m t j", t=PACK)
+                    if cut:
+                        nc.vector.tensor_copy(dst[:, :cut], src[:, :cut])
+                    nc.scalar.copy(dst[:, cut:], src[:, cut:])
+            codes = sbuf(f"w1_codes{z}", [P, H], U32)
+            plane = sbuf(f"w1_plane{z}", [P, H], U8)
+            nc.vector.quantize_mx(out=codes[:].bitcast(FP8X4), scales=plane[:], in_=grouped[:])
+            w1_codes.append(codes)
+            w1_planes.append(plane)
+
+        banks = {}
+        for t in range(PACK):
+            for h in range(2):
+                banks[t, h] = psum.tile([P, HALF], F32, name=f"first{t}{h}", tag=f"bank{2 * t + h}")
+
+        def first_product(z, t, h):
+            rows = slice(t * P, (t + 1) * P)
+            cols = slice(h * HALF, (h + 1) * HALF)
+            nc.tensor.matmul_mx(
+                out=banks[t, h][:],
+                lhsT=w1_codes[z][:, rows].bitcast(FP8X4),
+                lhsT_scale=w1_planes[z][:, rows],
+                rhs=(x_codes0[:, cols] if z == 0 else x_codes1[h][:]).bitcast(FP8X4),
+                rhs_scale=x_planes[4 * z : P, cols],
+                start=(z == 0),
+                stop=(z == PASSES - 1),
+            )
+
+        for t in range(PACK):
+            for h in range(2):
+                first_product(0, t, h)
+        for h in range(2):
+            nc.vector.tensor_copy(x_codes1[h][:], x_all[1][:].indirect(entries(h * HALF, HALF)))
+        order = [(0, 0), (1, 0), (0, 1), (1, 1), (2, 0), (2, 1), (3, 0), (3, 1)]
+        for t, h in order:
+            first_product(1, t, h)
+        product = {}
+        for t in range(PACK):
+            for h in range(2):
+                product[t, h] = sbuf(f"product{t}{h}", [P, HALF], F32)
+                nc.scalar.copy(product[t, h][:], banks[t, h][:])
+
+        hidden_low = [sbuf(f"hidden_low{h}", [P, 2, HALF], F32) for h in range(2)]
+        h_grouped = [sbuf(f"h_grouped{c}", [P, PACK * CHUNK], BF16) for c in range(CHUNKS)]
+
+        def add_position(target, t, first, count):
+            h, at = divmod(first, HALF)
+            nc.vector.tensor_tensor(
+                target, pe_all[t][:].indirect(entries(first, count)), product[t, h][:, at : at + count], ADD
+            )
+
+        def round_pair(copy, u, c, pair):
+            dst = h_grouped[c][:].rearrange("p (g i t) -> p g t i", i=4, t=PACK)
+            copy(dst[:, :, 2 * u : 2 * u + 2, :], pair.rearrange("p t (g i) -> p g t i", i=4))
+
+        for h in range(2):
+            add_position(hidden_low[h][:, 0, :], 0, h * HALF, HALF)
+        for h in range(2):
+            add_position(hidden_low[h][:, 1, :], 1, h * HALF, HALF)
+            for k in range(2):
+                round_pair(nc.scalar.copy, 0, 2 * h + k, hidden_low[h][:, :, k * CHUNK : (k + 1) * CHUNK])
         out_rows = out.rearrange("(b p) s -> p b s", p=P)
-        h_grouped0 = keep.tile([P, PACK * 128], BF16, name="h_grouped0", align_bytes=64)
-        nc.vector.tensor_tensor(
-            h_grouped0[:].rearrange("p (g i t) -> p g t i", i=2, t=PACK),
-            h_banks[0][:, :, 0:128].rearrange("p t (g i) -> p g t i", i=2),
-            picked[:, :, 0:128].rearrange("p t (g i) -> p g t i", i=2),
-            ADD,
-        )
-        h_grouped1 = keep.tile([P, PACK * 128], BF16, name="h_grouped1", align_bytes=64)
-        nc.vector.tensor_tensor(
-            h_grouped1[:].rearrange("p (g i t) -> p g t i", i=2, t=PACK),
-            h_banks[1][:, :, 0:128].rearrange("p t (g i) -> p g t i", i=2),
-            picked[:, :, 128:256].rearrange("p t (g i) -> p g t i", i=2),
-            ADD,
-        )
-        h_codes0 = keep.tile([P, 128], U32, name="h_codes0", align_bytes=64)
-        h_plane0 = keep.tile([P, 128], U8, name="h_plane0", align_bytes=64)
-        nc.vector.quantize_mx(out=h_codes0[:].bitcast(FP8X4), scales=h_plane0[:], in_=h_grouped0[:])
-        ob = psum.tile([P, 2, 128], F32, name="ob0", tag="out_bank0")
-        nc.tensor.matmul_mx(out=ob[:, 0, :], lhsT=w2_codes[:, 0:128].bitcast(FP8X4), lhsT_scale=w2_scale_rows[:, 0:128], rhs=h_codes0[:].bitcast(FP8X4), rhs_scale=h_plane0[:], start=True, stop=True)
-        nc.tensor.matmul_mx(out=ob[:, 1, :], lhsT=w2_codes[:, 128:256].bitcast(FP8X4), lhsT_scale=w2_scale_rows[:, 128:256], rhs=h_codes0[:].bitcast(FP8X4), rhs_scale=h_plane0[:], start=True, stop=True)
-        result0 = keep.tile([P, 2, 128], F32, name="result0", align_bytes=64)
-        nc.scalar.copy(result0[:], ob[:])
-        nc.sync.dma_start(out_rows[:, :, 0:128], result0[:])
-        h_grouped2 = keep.tile([P, PACK * 128], BF16, name="h_grouped2", align_bytes=64)
-        nc.vector.tensor_tensor(
-            h_grouped2[:].rearrange("p (g i t) -> p g t i", i=2, t=PACK),
-            h_banks[2][:, :, 0:128].rearrange("p t (g i) -> p g t i", i=2),
-            picked[:, :, 256:384].rearrange("p t (g i) -> p g t i", i=2),
-            ADD,
-        )
-        h_codes1 = keep.tile([P, 128], U32, name="h_codes1", align_bytes=64)
-        h_plane1 = keep.tile([P, 128], U8, name="h_plane1", align_bytes=64)
-        nc.vector.quantize_mx(out=h_codes1[:].bitcast(FP8X4), scales=h_plane1[:], in_=h_grouped1[:])
-        ob = psum.tile([P, 2, 128], F32, name="ob1", tag="out_bank1")
-        nc.tensor.matmul_mx(out=ob[:, 0, :], lhsT=w2_codes[:, 0:128].bitcast(FP8X4), lhsT_scale=w2_scale_rows[:, 0:128], rhs=h_codes1[:].bitcast(FP8X4), rhs_scale=h_plane1[:], start=True, stop=True)
-        nc.tensor.matmul_mx(out=ob[:, 1, :], lhsT=w2_codes[:, 128:256].bitcast(FP8X4), lhsT_scale=w2_scale_rows[:, 128:256], rhs=h_codes1[:].bitcast(FP8X4), rhs_scale=h_plane1[:], start=True, stop=True)
-        result1 = keep.tile([P, 2, 128], F32, name="result1", align_bytes=64)
-        nc.scalar.copy(result1[:], ob[:])
-        nc.sync.dma_start(out_rows[:, :, 128:256], result1[:])
-        h_grouped3 = keep.tile([P, PACK * 128], BF16, name="h_grouped3", align_bytes=64)
-        nc.vector.tensor_tensor(
-            h_grouped3[:].rearrange("p (g i t) -> p g t i", i=2, t=PACK),
-            h_banks[3][:, :, 0:128].rearrange("p t (g i) -> p g t i", i=2),
-            picked[:, :, 384:512].rearrange("p t (g i) -> p g t i", i=2),
-            ADD,
-        )
-        h_codes2 = keep.tile([P, 128], U32, name="h_codes2", align_bytes=64)
-        h_plane2 = keep.tile([P, 128], U8, name="h_plane2", align_bytes=64)
-        nc.vector.quantize_mx(out=h_codes2[:].bitcast(FP8X4), scales=h_plane2[:], in_=h_grouped2[:])
-        ob = psum.tile([P, 2, 128], F32, name="ob2", tag="h_bank0")
-        nc.tensor.matmul_mx(out=ob[:, 0, :], lhsT=w2_codes[:, 0:128].bitcast(FP8X4), lhsT_scale=w2_scale_rows[:, 0:128], rhs=h_codes2[:].bitcast(FP8X4), rhs_scale=h_plane2[:], start=True, stop=True)
-        nc.tensor.matmul_mx(out=ob[:, 1, :], lhsT=w2_codes[:, 128:256].bitcast(FP8X4), lhsT_scale=w2_scale_rows[:, 128:256], rhs=h_codes2[:].bitcast(FP8X4), rhs_scale=h_plane2[:], start=True, stop=True)
-        result2 = keep.tile([P, 2, 128], F32, name="result2", align_bytes=64)
-        nc.scalar.copy(result2[:], ob[:])
-        nc.sync.dma_start(out_rows[:, :, 256:384], result2[:])
-        h_codes3 = keep.tile([P, 128], U32, name="h_codes3", align_bytes=64)
-        h_plane3 = keep.tile([P, 128], U8, name="h_plane3", align_bytes=64)
-        nc.vector.quantize_mx(out=h_codes3[:].bitcast(FP8X4), scales=h_plane3[:], in_=h_grouped3[:])
-        ob = psum.tile([P, 128], F32, name="obl0", tag="out_last0")
-        nc.tensor.matmul_mx(out=ob[:], lhsT=w2_codes[:, 0:128].bitcast(FP8X4), lhsT_scale=w2_scale_rows[:, 0:128], rhs=h_codes3[:].bitcast(FP8X4), rhs_scale=h_plane3[:], start=True, stop=True)
-        resl0 = keep.tile([P, 128], F32, name="resl0", align_bytes=64)
-        nc.scalar.copy(resl0[:], ob[:])
-        nc.scalar.dma_start(out_rows[:, 0, 384:512], resl0[:])
-        ob = psum.tile([P, 128], F32, name="obl1", tag="out_last1")
-        nc.tensor.matmul_mx(out=ob[:], lhsT=w2_codes[:, 128:256].bitcast(FP8X4), lhsT_scale=w2_scale_rows[:, 128:256], rhs=h_codes3[:].bitcast(FP8X4), rhs_scale=h_plane3[:], start=True, stop=True)
-        resl1 = keep.tile([P, 128], F32, name="resl1", align_bytes=64)
-        nc.vector.tensor_copy(resl1[:], ob[:])
-        nc.sync.dma_start(out_rows[:, 1, 384:512], resl1[:])
+        ring = CHUNKS - 1
+        hidden_high = [sbuf(f"hidden_high{c}", [P, 2, CHUNK], F32) for c in range(ring)]
+        for c in range(ring):
+            add_position(hidden_high[c][:, 0, :], 2, c * CHUNK, CHUNK)
+        for c in range(ring):
+            add_position(hidden_high[c][:, 1, :], 3, c * CHUNK, CHUNK)
+            round_pair(nc.scalar.copy, 1, c, hidden_high[c][:])
+        for c in range(CHUNKS):
+            if c == 1:
+                last = sbuf("hidden_last", [P, 2, CHUNK], F32, tag="hidden_high0")
+                for t in (2, 3):
+                    add_position(last[:, t - 2, :], t, ring * CHUNK, CHUNK)
+            if c == 2:
+                round_pair(nc.vector.tensor_copy, 1, ring, last[:])
+            cols = slice(c * CHUNK, (c + 1) * CHUNK)
+            h_codes = sbuf(f"h_codes{c}", [P, CHUNK], U32)
+            h_plane = sbuf(f"h_plane{c}", [P, CHUNK], U8)
+            nc.vector.quantize_mx(
+                out=h_codes[:].bitcast(FP8X4),
+                scales=h_plane[:],
+                in_=h_grouped[c][:],
+            )
+
+            def second_product(target, b):
+                nc.tensor.matmul_mx(
+                    out=target,
+                    lhsT=w2_codes[:, b * P : (b + 1) * P].bitcast(FP8X4),
+                    lhsT_scale=w2_scale_rows[:, b * P : (b + 1) * P],
+                    rhs=h_codes[:].bitcast(FP8X4),
+                    rhs_scale=h_plane[:],
+                    start=True,
+                    stop=True,
+                )
+
+            if c < CHUNKS - 1:
+                bank = psum.tile([P, 2, CHUNK], F32, name=f"second{c}", tag=f"bank{c}")
+                for b in range(2):
+                    second_product(bank[:, b, :], b)
+                result = sbuf(f"result{c}", [P, 2, CHUNK], F32)
+                nc.scalar.copy(result[:], bank[:])
+                nc.sync.dma_start(out_rows[:, :, cols], result[:])
+            else:
+                for b, (copy, queue) in enumerate(((nc.scalar.copy, nc.scalar), (nc.vector.tensor_copy, nc.sync))):
+                    bank = psum.tile([P, CHUNK], F32, name=f"last{b}", tag=f"bank{c + b}")
+                    second_product(bank[:], b)
+                    result = sbuf(f"result_last{b}", [P, CHUNK], F32)
+                    copy(result[:], bank[:])
+                    queue.dma_start(out_rows[:, b, cols], result[:])

@@ -46,8 +46,8 @@ def tile_picked_posadd_none_p_kernel(
         pe_rows = pe.rearrange("(p t) c -> p t c", t=PACK)
         w1_rows = w1.rearrange("(z p j) c -> z p j c", p=P, j=PACK)
         x_all = [sbuf(f"x_all{z}", [P, T], U32) for z in range(PASSES)]
-        pieces = [(0, 0, 2, 32), (0, 2, 4, 80), (1, 0, 2, 0), (1, 2, 4, 104)]
-        w1_raw = [sbuf(f"w1_raw{i}", [P, j1 - j0, H], F32) for i, (z, j0, j1, cut) in enumerate(pieces)]
+        pieces = [(0, 0, 2), (0, 2, 4), (1, 0, 2), (1, 2, 4)]
+        w1_raw = [sbuf(f"w1_raw{i}", [P, j1 - j0, H], F32) for i, (z, j0, j1) in enumerate(pieces)]
         pe_all = [sbuf(f"pe_all{t}", [P, T], F32) for t in range(PACK)]
         w2_codes = sbuf("w2_codes", [P, N], U32)
 
@@ -60,7 +60,7 @@ def tile_picked_posadd_none_p_kernel(
             nc.sync.dma_start(
                 x_scale_rows[32 * q : 32 * q + 8, :].bitcast(I32), x_scales[:, 4 * q : 4 * q + 4, :].bitcast(I32)
             )
-        for raw, (z, j0, j1, cut) in zip(w1_raw, pieces):
+        for raw, (z, j0, j1) in zip(w1_raw, pieces):
             nc.sync.dma_start(raw[:], w1_rows[z, :, j0:j1, :])
         load_words(x_all[1], x_words[1])
         for t in range(PACK):
@@ -73,57 +73,70 @@ def tile_picked_posadd_none_p_kernel(
 
         x_planes = sbuf("x_planes", [P, S], U8)
         x_codes0 = sbuf("x_codes0", [P, S], U32)
-        x_codes1 = [sbuf(f"x_codes1{h}", [P, HALF], U32) for h in range(2)]
+        x_codes1 = sbuf("x_codes1", [P, S], U32)
         nc.vector.tensor_copy(x_codes0[:], x_all[0][:].indirect(offsets[:]))
         nc.vector.tensor_copy(x_planes[:], x_scale_rows[:].indirect(offsets[:]))
 
-        w1_codes, w1_planes = [], []
-        for z in range(PASSES):
-            grouped = sbuf(f"w1_grouped{z}", [P, PACK * H], BF16)
-            for raw, (piece_z, j0, j1, cut) in zip(w1_raw, pieces):
-                if piece_z == z:
-                    dst = grouped[:].rearrange("p (t m j) -> p m t j", t=PACK, j=PACK)[:, :, :, j0:j1]
-                    src = raw[:].rearrange("p j (m t) -> p m t j", t=PACK)
-                    if cut:
-                        nc.vector.tensor_copy(dst[:, :cut], src[:, :cut])
-                    nc.scalar.copy(dst[:, cut:], src[:, cut:])
-            codes = sbuf(f"w1_codes{z}", [P, H], U32)
-            plane = sbuf(f"w1_plane{z}", [P, H], U8)
-            nc.vector.quantize_mx(out=codes[:].bitcast(FP8X4), scales=plane[:], in_=grouped[:])
-            w1_codes.append(codes)
-            w1_planes.append(plane)
+        w1_grouped = [sbuf(f"w1_grouped{z}", [P, PACK * H], BF16) for z in range(PASSES)]
+        w1_codes = [sbuf(f"w1_codes{z}", [P, H], U32) for z in range(PASSES)]
+        w1_planes = [sbuf(f"w1_plane{z}", [P, H], U8) for z in range(PASSES)]
 
+        def round_w1(i, copy, columns, planes):
+            z, j0, j1 = pieces[i]
+            dst = w1_grouped[z][:].rearrange("p (t m j) -> p m t j", t=PACK, j=PACK)[:, columns, planes, j0:j1]
+            copy(dst, w1_raw[i][:].rearrange("p j (m t) -> p m t j", t=PACK)[:, columns, planes, :])
+
+        def quantise_w1(z, t0, t1):
+            nc.vector.quantize_mx(
+                out=w1_codes[z][:, t0 * P : t1 * P].bitcast(FP8X4),
+                scales=w1_planes[z][:, t0 * P : t1 * P],
+                in_=w1_grouped[z][:, t0 * H : t1 * H],
+            )
+
+        every = slice(None)
+        round_w1(0, nc.scalar.copy, every, every)
+        round_w1(1, nc.vector.tensor_copy, every, every)
+        quantise_w1(0, 0, 4)
+        round_w1(2, nc.vector.tensor_copy, slice(0, 56), every)
+        round_w1(2, nc.scalar.copy, slice(56, P), every)
+        round_w1(3, nc.vector.tensor_copy, every, slice(0, 2))
+        round_w1(3, nc.vector.tensor_copy, slice(0, 64), slice(2, 4))
+        round_w1(3, nc.scalar.copy, slice(64, P), slice(2, 4))
+        quantise_w1(1, 0, 2)
+        quantise_w1(1, 2, 4)
+        for first, count in ((0, CHUNK), (CHUNK, CHUNK), (HALF, HALF)):
+            nc.vector.tensor_copy(x_codes1[:, first : first + count], x_all[1][:].indirect(entries(first, count)))
+
+        units = [(0, 0, CHUNK), (0, CHUNK, CHUNK), (1, 0, HALF), (0, HALF, HALF), (1, HALF, HALF)]
+        early = len(units)
+        units = units + [(t, h * HALF, HALF) for t in (2, 3) for h in range(2)]
         banks = {}
-        for t in range(PACK):
-            for h in range(2):
-                banks[t, h] = psum.tile([P, HALF], F32, name=f"first{t}{h}", tag=f"bank{2 * t + h}")
 
-        def first_product(z, t, h):
+        def first_product(z, i):
+            t, first, count = units[i]
+            if z == 0:
+                banks[i] = psum.tile([P, count], F32, name=f"first{i}", tag=f"bank{i % early}")
             rows = slice(t * P, (t + 1) * P)
-            cols = slice(h * HALF, (h + 1) * HALF)
+            cols = slice(first, first + count)
             nc.tensor.matmul_mx(
-                out=banks[t, h][:],
+                out=banks[i][:],
                 lhsT=w1_codes[z][:, rows].bitcast(FP8X4),
                 lhsT_scale=w1_planes[z][:, rows],
-                rhs=(x_codes0[:, cols] if z == 0 else x_codes1[h][:]).bitcast(FP8X4),
+                rhs=(x_codes0 if z == 0 else x_codes1)[:, cols].bitcast(FP8X4),
                 rhs_scale=x_planes[4 * z : P, cols],
                 start=(z == 0),
                 stop=(z == PASSES - 1),
             )
 
-        for t in range(PACK):
-            for h in range(2):
-                first_product(0, t, h)
-        for h in range(2):
-            nc.vector.tensor_copy(x_codes1[h][:], x_all[1][:].indirect(entries(h * HALF, HALF)))
-        order = [(0, 0), (1, 0), (0, 1), (1, 1), (2, 0), (2, 1), (3, 0), (3, 1)]
-        for t, h in order:
-            first_product(1, t, h)
-        product = {}
-        for t in range(PACK):
-            for h in range(2):
-                product[t, h] = sbuf(f"product{t}{h}", [P, HALF], F32)
-                nc.scalar.copy(product[t, h][:], banks[t, h][:])
+        product = {(t, h): sbuf(f"product{t}{h}", [P, HALF], F32) for t in range(PACK) for h in range(2)}
+        for i in range(early):
+            first_product(0, i)
+        for i, (t, first, count) in enumerate(units):
+            if i >= early:
+                first_product(0, i)
+            first_product(1, i)
+            h, at = divmod(first, HALF)
+            nc.scalar.copy(product[t, h][:, at : at + count], banks[i][:])
 
         hidden_low = [sbuf(f"hidden_low{h}", [P, 2, HALF], F32) for h in range(2)]
         h_grouped = [sbuf(f"h_grouped{c}", [P, PACK * CHUNK], BF16) for c in range(CHUNKS)]
@@ -138,9 +151,11 @@ def tile_picked_posadd_none_p_kernel(
             dst = h_grouped[c][:].rearrange("p (g i t) -> p g t i", i=4, t=PACK)
             copy(dst[:, :, 2 * u : 2 * u + 2, :], pair.rearrange("p t (g i) -> p g t i", i=4))
 
+        for k in range(2):
+            add_position(hidden_low[0][:, 0, k * CHUNK : (k + 1) * CHUNK], 0, k * CHUNK, CHUNK)
         for h in range(2):
-            add_position(hidden_low[h][:, 0, :], 0, h * HALF, HALF)
-        for h in range(2):
+            if h == 1:
+                add_position(hidden_low[h][:, 0, :], 0, HALF, HALF)
             add_position(hidden_low[h][:, 1, :], 1, h * HALF, HALF)
             for k in range(2):
                 round_pair(nc.scalar.copy, 0, 2 * h + k, hidden_low[h][:, :, k * CHUNK : (k + 1) * CHUNK])
@@ -180,7 +195,7 @@ def tile_picked_posadd_none_p_kernel(
                 )
 
             if c < CHUNKS - 1:
-                bank = psum.tile([P, 2, CHUNK], F32, name=f"second{c}", tag=f"bank{c}")
+                bank = psum.tile([P, 2, CHUNK], F32, name=f"second{c}", tag=f"bank{5 + c}")
                 for b in range(2):
                     second_product(bank[:, b, :], b)
                 result = sbuf(f"result{c}", [P, 2, CHUNK], F32)
@@ -188,7 +203,7 @@ def tile_picked_posadd_none_p_kernel(
                 nc.sync.dma_start(out_rows[:, :, cols], result[:])
             else:
                 for b, (copy, queue) in enumerate(((nc.scalar.copy, nc.scalar), (nc.vector.tensor_copy, nc.sync))):
-                    bank = psum.tile([P, CHUNK], F32, name=f"last{b}", tag=f"bank{c + b}")
+                    bank = psum.tile([P, CHUNK], F32, name=f"last{b}", tag=f"bank{4 * b}")
                     second_product(bank[:], b)
                     result = sbuf(f"result_last{b}", [P, CHUNK], F32)
                     copy(result[:], bank[:])

@@ -56,12 +56,14 @@ def tile_picked_posadd_none_p_kernel(
 
         load_words(x_all[0], x_words[0])
         nc.sync.dma_start(offsets[:], offs)
-        for q in range(4):
-            nc.sync.dma_start(
-                x_scale_rows[32 * q : 32 * q + 8, :].bitcast(I32), x_scales[:, 4 * q : 4 * q + 4, :].bitcast(I32)
-            )
-        for raw, (z, j0, j1) in zip(w1_raw, pieces):
-            nc.sync.dma_start(raw[:], w1_rows[z, :, j0:j1, :])
+        for i, (z, j0, j1) in enumerate(pieces):
+            nc.sync.dma_start(w1_raw[i][:], w1_rows[z, :, j0:j1, :])
+            if i == 0:
+                for q in range(4):
+                    nc.sync.dma_start(
+                        x_scale_rows[32 * q : 32 * q + 8, :].bitcast(I32),
+                        x_scales[:, 4 * q : 4 * q + 4, :].bitcast(I32),
+                    )
         load_words(x_all[1], x_words[1])
         for t in range(PACK):
             nc.sync.dma_start(pe_all[t][:], pe_rows[:, t, :])
@@ -94,32 +96,33 @@ def tile_picked_posadd_none_p_kernel(
             )
 
         every = slice(None)
-        round_w1(0, nc.scalar.copy, every, every)
-        round_w1(1, nc.vector.tensor_copy, every, every)
+        round_w1(0, nc.vector.tensor_copy, slice(0, 32), every)
+        round_w1(0, nc.scalar.copy, slice(32, P), every)
+        round_w1(1, nc.vector.tensor_copy, slice(0, 80), every)
+        round_w1(1, nc.scalar.copy, slice(80, P), every)
         quantise_w1(0, 0, 4)
         round_w1(2, nc.vector.tensor_copy, slice(0, 56), every)
         round_w1(2, nc.scalar.copy, slice(56, P), every)
-        round_w1(3, nc.vector.tensor_copy, every, slice(0, 2))
-        round_w1(3, nc.vector.tensor_copy, slice(0, 64), slice(2, 4))
-        round_w1(3, nc.scalar.copy, slice(64, P), slice(2, 4))
+        round_w1(3, nc.vector.tensor_copy, slice(0, 96), slice(0, 2))
+        round_w1(3, nc.scalar.copy, slice(96, P), slice(0, 2))
+        round_w1(3, nc.vector.tensor_copy, slice(0, 56), slice(2, 4))
+        round_w1(3, nc.scalar.copy, slice(56, P), slice(2, 4))
         quantise_w1(1, 0, 2)
         quantise_w1(1, 2, 4)
-        for first, count in ((0, CHUNK), (CHUNK, CHUNK), (HALF, HALF)):
-            nc.vector.tensor_copy(x_codes1[:, first : first + count], x_all[1][:].indirect(entries(first, count)))
+        for h in range(2):
+            nc.vector.tensor_copy(x_codes1[:, h * HALF : (h + 1) * HALF], x_all[1][:].indirect(entries(h * HALF, HALF)))
 
-        units = [(0, 0, CHUNK), (0, CHUNK, CHUNK), (1, 0, HALF), (0, HALF, HALF), (1, HALF, HALF)]
-        early = len(units)
-        units = units + [(t, h * HALF, HALF) for t in (2, 3) for h in range(2)]
-        banks = {}
+        banks = {
+            (t, h): psum.tile([P, HALF], F32, name=f"first{t}{h}", tag=f"bank{2 * t + h}")
+            for t in range(PACK)
+            for h in range(2)
+        }
 
-        def first_product(z, i):
-            t, first, count = units[i]
-            if z == 0:
-                banks[i] = psum.tile([P, count], F32, name=f"first{i}", tag=f"bank{i % early}")
+        def first_product(z, t, h):
             rows = slice(t * P, (t + 1) * P)
-            cols = slice(first, first + count)
+            cols = slice(h * HALF, (h + 1) * HALF)
             nc.tensor.matmul_mx(
-                out=banks[i][:],
+                out=banks[t, h][:],
                 lhsT=w1_codes[z][:, rows].bitcast(FP8X4),
                 lhsT_scale=w1_planes[z][:, rows],
                 rhs=(x_codes0 if z == 0 else x_codes1)[:, cols].bitcast(FP8X4),
@@ -128,52 +131,50 @@ def tile_picked_posadd_none_p_kernel(
                 stop=(z == PASSES - 1),
             )
 
-        product = {(t, h): sbuf(f"product{t}{h}", [P, HALF], F32) for t in range(PACK) for h in range(2)}
-        for i in range(early):
-            first_product(0, i)
-        for i, (t, first, count) in enumerate(units):
-            if i >= early:
-                first_product(0, i)
-            first_product(1, i)
-            h, at = divmod(first, HALF)
-            nc.scalar.copy(product[t, h][:, at : at + count], banks[i][:])
+        product = {t: sbuf(f"product{t}", [P, S], F32) for t in range(1, PACK)}
+        for z in range(PASSES):
+            for t in range(PACK):
+                for h in range(2):
+                    first_product(z, t, h)
+                    if z == PASSES - 1 and t > 0:
+                        nc.scalar.copy(product[t][:, h * HALF : (h + 1) * HALF], banks[t, h][:])
 
-        hidden_low = [sbuf(f"hidden_low{h}", [P, 2, HALF], F32) for h in range(2)]
+        hidden_low = sbuf("hidden_low", [P, 2, S], F32)
         h_grouped = [sbuf(f"h_grouped{c}", [P, PACK * CHUNK], BF16) for c in range(CHUNKS)]
 
         def add_position(target, t, first, count):
-            h, at = divmod(first, HALF)
             nc.vector.tensor_tensor(
-                target, pe_all[t][:].indirect(entries(first, count)), product[t, h][:, at : at + count], ADD
+                target, pe_all[t][:].indirect(entries(first, count)), product[t][:, first : first + count], ADD
             )
 
         def round_pair(copy, u, c, pair):
             dst = h_grouped[c][:].rearrange("p (g i t) -> p g t i", i=4, t=PACK)
             copy(dst[:, :, 2 * u : 2 * u + 2, :], pair.rearrange("p t (g i) -> p g t i", i=4))
 
-        for k in range(2):
-            add_position(hidden_low[0][:, 0, k * CHUNK : (k + 1) * CHUNK], 0, k * CHUNK, CHUNK)
+        picked = sbuf("picked", [P, S], F32)
         for h in range(2):
-            if h == 1:
-                add_position(hidden_low[h][:, 0, :], 0, HALF, HALF)
-            add_position(hidden_low[h][:, 1, :], 1, h * HALF, HALF)
-            for k in range(2):
-                round_pair(nc.scalar.copy, 0, 2 * h + k, hidden_low[h][:, :, k * CHUNK : (k + 1) * CHUNK])
+            nc.vector.tensor_copy(picked[:, h * HALF : (h + 1) * HALF], pe_all[0][:].indirect(entries(h * HALF, HALF)))
+        for h in range(2):
+            cols = slice(h * HALF, (h + 1) * HALF)
+            nc.vector.tensor_tensor(hidden_low[:, 0, cols], banks[0, h][:], picked[:, cols], ADD)
+        for h in range(2):
+            add_position(hidden_low[:, 1, h * HALF : (h + 1) * HALF], 1, h * HALF, HALF)
+            for c in (2 * h, 2 * h + 1):
+                round_pair(nc.scalar.copy, 0, c, hidden_low[:, :, c * CHUNK : (c + 1) * CHUNK])
         out_rows = out.rearrange("(b p) s -> p b s", p=P)
         ring = CHUNKS - 1
-        hidden_high = [sbuf(f"hidden_high{c}", [P, 2, CHUNK], F32) for c in range(ring)]
+        hidden_high = sbuf("hidden_high", [P, 2, ring * CHUNK], F32)
+        add_position(hidden_high[:, 0, :], 2, 0, ring * CHUNK)
         for c in range(ring):
-            add_position(hidden_high[c][:, 0, :], 2, c * CHUNK, CHUNK)
-        for c in range(ring):
-            add_position(hidden_high[c][:, 1, :], 3, c * CHUNK, CHUNK)
-            round_pair(nc.scalar.copy, 1, c, hidden_high[c][:])
+            cols = slice(c * CHUNK, (c + 1) * CHUNK)
+            add_position(hidden_high[:, 1, cols], 3, c * CHUNK, CHUNK)
+            round_pair(nc.scalar.copy, 1, c, hidden_high[:, :, cols])
         for c in range(CHUNKS):
             if c == 1:
-                last = sbuf("hidden_last", [P, 2, CHUNK], F32, tag="hidden_high0")
                 for t in (2, 3):
-                    add_position(last[:, t - 2, :], t, ring * CHUNK, CHUNK)
+                    add_position(hidden_high[:, t - 2, :CHUNK], t, ring * CHUNK, CHUNK)
             if c == 2:
-                round_pair(nc.vector.tensor_copy, 1, ring, last[:])
+                round_pair(nc.vector.tensor_copy, 1, ring, hidden_high[:, :, :CHUNK])
             cols = slice(c * CHUNK, (c + 1) * CHUNK)
             h_codes = sbuf(f"h_codes{c}", [P, CHUNK], U32)
             h_plane = sbuf(f"h_plane{c}", [P, CHUNK], U8)
@@ -195,15 +196,15 @@ def tile_picked_posadd_none_p_kernel(
                 )
 
             if c < CHUNKS - 1:
-                bank = psum.tile([P, 2, CHUNK], F32, name=f"second{c}", tag=f"bank{5 + c}")
+                bank = psum.tile([P, 2, CHUNK], F32, name=f"second{c}", tag=f"bank{c}")
                 for b in range(2):
                     second_product(bank[:, b, :], b)
                 result = sbuf(f"result{c}", [P, 2, CHUNK], F32)
                 nc.scalar.copy(result[:], bank[:])
                 nc.sync.dma_start(out_rows[:, :, cols], result[:])
             else:
-                for b, (copy, queue) in enumerate(((nc.scalar.copy, nc.scalar), (nc.vector.tensor_copy, nc.sync))):
-                    bank = psum.tile([P, CHUNK], F32, name=f"last{b}", tag=f"bank{4 * b}")
+                for b, (copy, queue) in enumerate(((nc.vector.tensor_copy, nc.sync), (nc.scalar.copy, nc.scalar))):
+                    bank = psum.tile([P, CHUNK], F32, name=f"last{b}", tag=f"bank{3 + b}")
                     second_product(bank[:], b)
                     result = sbuf(f"result_last{b}", [P, CHUNK], F32)
                     copy(result[:], bank[:])

@@ -109,8 +109,7 @@ def tile_picked_posadd_none_p_kernel(
         round_w1(3, nc.scalar.copy, slice(56, P), slice(2, 4))
         quantise_w1(1, 0, 2)
         quantise_w1(1, 2, 4)
-        for h in range(2):
-            nc.vector.tensor_copy(x_codes1[:, h * HALF : (h + 1) * HALF], x_all[1][:].indirect(entries(h * HALF, HALF)))
+        nc.vector.tensor_copy(x_codes1[:], x_all[1][:].indirect(offsets[:]))
 
         banks = {
             (t, h): psum.tile([P, HALF], F32, name=f"first{t}{h}", tag=f"bank{2 * t + h}")
@@ -133,18 +132,21 @@ def tile_picked_posadd_none_p_kernel(
 
         product = {t: sbuf(f"product{t}", [P, S], F32) for t in range(1, PACK)}
         for z in range(PASSES):
-            for t in range(PACK):
+            for pair in range(2):
                 for h in range(2):
-                    first_product(z, t, h)
-                    if z == PASSES - 1 and t > 0:
-                        nc.scalar.copy(product[t][:, h * HALF : (h + 1) * HALF], banks[t, h][:])
+                    for t in (2 * pair, 2 * pair + 1):
+                        first_product(z, t, h)
+                        if z == PASSES - 1 and t > 0:
+                            count = CHUNK if (t, h) == (2, 1) else HALF
+                            nc.scalar.copy(product[t][:, h * HALF : h * HALF + count], banks[t, h][:, :count])
 
         hidden_low = sbuf("hidden_low", [P, 2, S], F32)
         h_grouped = [sbuf(f"h_grouped{c}", [P, PACK * CHUNK], BF16) for c in range(CHUNKS)]
 
-        def add_position(target, t, first, count):
+        def add_position(target, t, first, count, at=None):
+            at = first if at is None else at
             nc.vector.tensor_tensor(
-                target, pe_all[t][:].indirect(entries(first, count)), product[t][:, first : first + count], ADD
+                target, pe_all[t][:].indirect(entries(first, count)), product[t][:, at : at + count], ADD
             )
 
         def round_pair(copy, u, c, pair):
@@ -165,14 +167,26 @@ def tile_picked_posadd_none_p_kernel(
         ring = CHUNKS - 1
         hidden_high = sbuf("hidden_high", [P, 2, ring * CHUNK], F32)
         add_position(hidden_high[:, 0, :], 2, 0, ring * CHUNK)
+        nc.scalar.copy(product[2][:, :CHUNK], banks[2, 1][:, CHUNK:])
+        warm = psum.tile([P, S], F32, name="warm", tag="bank5")
+        for z in range(PASSES):
+            nc.tensor.matmul_mx(
+                out=warm[:],
+                lhsT=w1_codes[z][:, :P].bitcast(FP8X4),
+                lhsT_scale=w1_planes[z][:, :P],
+                rhs=(x_codes0 if z == 0 else x_codes1)[:].bitcast(FP8X4),
+                rhs_scale=x_planes[4 * z : P, :],
+                start=(z == 0),
+                stop=(z == PASSES - 1),
+            )
         for c in range(ring):
             cols = slice(c * CHUNK, (c + 1) * CHUNK)
             add_position(hidden_high[:, 1, cols], 3, c * CHUNK, CHUNK)
             round_pair(nc.scalar.copy, 1, c, hidden_high[:, :, cols])
         for c in range(CHUNKS):
             if c == 1:
-                for t in (2, 3):
-                    add_position(hidden_high[:, t - 2, :CHUNK], t, ring * CHUNK, CHUNK)
+                add_position(hidden_high[:, 0, :CHUNK], 2, ring * CHUNK, CHUNK, at=0)
+                add_position(hidden_high[:, 1, :CHUNK], 3, ring * CHUNK, CHUNK)
             if c == 2:
                 round_pair(nc.vector.tensor_copy, 1, ring, hidden_high[:, :, :CHUNK])
             cols = slice(c * CHUNK, (c + 1) * CHUNK)

@@ -98,8 +98,8 @@ def tile_picked_posadd_none_p_kernel(
         every = slice(None)
         round_w1(0, nc.vector.tensor_copy, slice(0, 32), every)
         round_w1(0, nc.scalar.copy, slice(32, P), every)
-        round_w1(1, nc.vector.tensor_copy, slice(0, 80), every)
-        round_w1(1, nc.scalar.copy, slice(80, P), every)
+        round_w1(1, nc.vector.tensor_copy, slice(0, 64), every)
+        round_w1(1, nc.scalar.copy, slice(64, P), every)
         quantise_w1(0, 0, 4)
         round_w1(2, nc.vector.tensor_copy, slice(0, 56), every)
         round_w1(2, nc.scalar.copy, slice(56, P), every)
@@ -150,8 +150,8 @@ def tile_picked_posadd_none_p_kernel(
             )
 
         def round_pair(copy, u, c, pair):
-            dst = h_grouped[c][:].rearrange("p (g i t) -> p g t i", i=4, t=PACK)
-            copy(dst[:, :, 2 * u : 2 * u + 2, :], pair.rearrange("p t (g i) -> p g t i", i=4))
+            dst = h_grouped[c][:].rearrange("p (g i t) -> p g t i", i=2, t=PACK)
+            copy(dst[:, :, 2 * u : 2 * u + 2, :], pair.rearrange("p t (g i) -> p g t i", i=2))
 
         picked = sbuf("picked", [P, S], F32)
         for h in range(2):

@@ -209,17 +209,20 @@ def tile_picked_posadd_none_p_kernel(
                     stop=True,
                 )
 
-            if c < CHUNKS - 1:
+            result = sbuf(f"result{c}", [P, 2, CHUNK], F32)
+            if c < CHUNKS - 2:
                 bank = psum.tile([P, 2, CHUNK], F32, name=f"second{c}", tag=f"bank{c}")
                 for b in range(2):
                     second_product(bank[:, b, :], b)
-                result = sbuf(f"result{c}", [P, 2, CHUNK], F32)
                 nc.scalar.copy(result[:], bank[:])
                 nc.sync.dma_start(out_rows[:, :, cols], result[:])
             else:
-                for b, (copy, queue) in enumerate(((nc.vector.tensor_copy, nc.sync), (nc.scalar.copy, nc.scalar))):
-                    bank = psum.tile([P, CHUNK], F32, name=f"last{b}", tag=f"bank{3 + b}")
+                for b, copy in enumerate((nc.vector.tensor_copy, nc.scalar.copy)):
+                    tag = ((2, 3), (4, 6))[c - 2][b]
+                    bank = psum.tile([P, CHUNK], F32, name=f"second{c}{b}", tag=f"bank{tag}")
                     second_product(bank[:], b)
-                    result = sbuf(f"result_last{b}", [P, CHUNK], F32)
-                    copy(result[:], bank[:])
-                    queue.dma_start(out_rows[:, b, cols], result[:])
+                    copy(result[:, b, :], bank[:])
+                    if c == CHUNKS - 1:
+                        (nc.sync, nc.scalar)[b].dma_start(out_rows[:, b, cols], result[:, b, :])
+                if c < CHUNKS - 1:
+                    nc.sync.dma_start(out_rows[:, :, cols], result[:])

@@ -222,7 +222,4 @@ def tile_picked_posadd_none_p_kernel(
                     bank = psum.tile([P, CHUNK], F32, name=f"second{c}{b}", tag=f"bank{tag}")
                     second_product(bank[:], b)
                     copy(result[:, b, :], bank[:])
-                    if c == CHUNKS - 1:
-                        (nc.sync, nc.scalar)[b].dma_start(out_rows[:, b, cols], result[:, b, :])
-                if c < CHUNKS - 1:
-                    nc.sync.dma_start(out_rows[:, :, cols], result[:])
+                nc.sync.dma_start(out_rows[:, :, cols], result[:])

@@ -168,17 +168,6 @@ def tile_picked_posadd_none_p_kernel(
         hidden_high = sbuf("hidden_high", [P, 2, ring * CHUNK], F32)
         add_position(hidden_high[:, 0, :], 2, 0, ring * CHUNK)
         nc.scalar.copy(product[2][:, :CHUNK], banks[2, 1][:, CHUNK:])
-        warm = psum.tile([P, S], F32, name="warm", tag="bank5")
-        for z in range(PASSES):
-            nc.tensor.matmul_mx(
-                out=warm[:],
-                lhsT=w1_codes[z][:, :P].bitcast(FP8X4),
-                lhsT_scale=w1_planes[z][:, :P],
-                rhs=(x_codes0 if z == 0 else x_codes1)[:].bitcast(FP8X4),
-                rhs_scale=x_planes[4 * z : P, :],
-                start=(z == 0),
-                stop=(z == PASSES - 1),
-            )
         for c in range(ring):
             cols = slice(c * CHUNK, (c + 1) * CHUNK)
             add_position(hidden_high[:, 1, cols], 3, c * CHUNK, CHUNK)

@@ -137,16 +137,14 @@ def tile_picked_posadd_none_p_kernel(
                     for t in (2 * pair, 2 * pair + 1):
                         first_product(z, t, h)
                         if z == PASSES - 1 and t > 0:
-                            count = CHUNK if (t, h) == (2, 1) else HALF
-                            nc.scalar.copy(product[t][:, h * HALF : h * HALF + count], banks[t, h][:, :count])
+                            nc.scalar.copy(product[t][:, h * HALF : (h + 1) * HALF], banks[t, h][:])
 
         hidden_low = sbuf("hidden_low", [P, 2, S], F32)
         h_grouped = [sbuf(f"h_grouped{c}", [P, PACK * CHUNK], BF16) for c in range(CHUNKS)]
 
-        def add_position(target, t, first, count, at=None):
-            at = first if at is None else at
+        def add_position(target, t, first, count):
             nc.vector.tensor_tensor(
-                target, pe_all[t][:].indirect(entries(first, count)), product[t][:, at : at + count], ADD
+                target, pe_all[t][:].indirect(entries(first, count)), product[t][:, first : first + count], ADD
             )
 
         def round_pair(copy, u, c, pair):
@@ -167,14 +165,13 @@ def tile_picked_posadd_none_p_kernel(
         ring = CHUNKS - 1
         hidden_high = sbuf("hidden_high", [P, 2, ring * CHUNK], F32)
         add_position(hidden_high[:, 0, :], 2, 0, ring * CHUNK)
-        nc.scalar.copy(product[2][:, :CHUNK], banks[2, 1][:, CHUNK:])
         for c in range(ring):
             cols = slice(c * CHUNK, (c + 1) * CHUNK)
             add_position(hidden_high[:, 1, cols], 3, c * CHUNK, CHUNK)
             round_pair(nc.scalar.copy, 1, c, hidden_high[:, :, cols])
         for c in range(CHUNKS):
             if c == 1:
-                add_position(hidden_high[:, 0, :CHUNK], 2, ring * CHUNK, CHUNK, at=0)
+                add_position(hidden_high[:, 0, :CHUNK], 2, ring * CHUNK, CHUNK)
                 add_position(hidden_high[:, 1, :CHUNK], 3, ring * CHUNK, CHUNK)
             if c == 2:
                 round_pair(nc.vector.tensor_copy, 1, ring, hidden_high[:, :, :CHUNK])
@@ -207,7 +204,7 @@ def tile_picked_posadd_none_p_kernel(
                 nc.sync.dma_start(out_rows[:, :, cols], result[:])
             else:
                 for b, copy in enumerate((nc.vector.tensor_copy, nc.scalar.copy)):
-                    tag = ((2, 3), (4, 6))[c - 2][b]
+                    tag = ((2, 3), (4, 5))[c - 2][b]
                     bank = psum.tile([P, CHUNK], F32, name=f"second{c}{b}", tag=f"bank{tag}")
                     second_product(bank[:], b)
                     copy(result[:, b, :], bank[:])

@@ -80,67 +80,60 @@ def tile_picked_posadd_none_p_kernel(
         nc.vector.tensor_copy(x_planes[:], x_scale_rows[:].indirect(offsets[:]))
 
         w1_grouped = [sbuf(f"w1_grouped{z}", [P, PACK * H], BF16) for z in range(PASSES)]
-        w1_codes = [sbuf(f"w1_codes{z}", [P, H], U32) for z in range(PASSES)]
-        w1_planes = [sbuf(f"w1_plane{z}", [P, H], U8) for z in range(PASSES)]
+        w1_codes, w1_planes = {}, {}
 
         def round_w1(i, copy, columns, planes):
             z, j0, j1 = pieces[i]
             dst = w1_grouped[z][:].rearrange("p (t m j) -> p m t j", t=PACK, j=PACK)[:, columns, planes, j0:j1]
             copy(dst, w1_raw[i][:].rearrange("p j (m t) -> p m t j", t=PACK)[:, columns, planes, :])
 
-        def quantise_w1(z, t0, t1):
-            nc.vector.quantize_mx(
-                out=w1_codes[z][:, t0 * P : t1 * P].bitcast(FP8X4),
-                scales=w1_planes[z][:, t0 * P : t1 * P],
-                in_=w1_grouped[z][:, t0 * H : t1 * H],
-            )
+        def quantise_w1(z, t0, t1, tag=None):
+            codes = sbuf(f"w1_codes{z}{t0}", [P, (t1 - t0) * P], U32, tag=tag)
+            plane = sbuf(f"w1_plane{z}{t0}", [P, (t1 - t0) * P], U8)
+            nc.vector.quantize_mx(out=codes[:].bitcast(FP8X4), scales=plane[:], in_=w1_grouped[z][:, t0 * H : t1 * H])
+            for t in range(t0, t1):
+                w1_codes[z, t] = codes[:, (t - t0) * P : (t - t0 + 1) * P]
+                w1_planes[z, t] = plane[:, (t - t0) * P : (t - t0 + 1) * P]
 
         every = slice(None)
-        round_w1(0, nc.vector.tensor_copy, slice(0, 32), every)
-        round_w1(0, nc.scalar.copy, slice(32, P), every)
-        round_w1(1, nc.vector.tensor_copy, slice(0, 64), every)
-        round_w1(1, nc.scalar.copy, slice(64, P), every)
+
+        def share(i, columns, planes=every):
+            if columns > 0:
+                round_w1(i, nc.vector.tensor_copy, slice(0, columns), planes)
+            round_w1(i, nc.scalar.copy, slice(columns, P), planes)
+
+        share(0, 32)
+        share(1, 64)
         quantise_w1(0, 0, 4)
-        round_w1(2, nc.vector.tensor_copy, slice(0, 56), every)
-        round_w1(2, nc.scalar.copy, slice(56, P), every)
-        round_w1(3, nc.vector.tensor_copy, slice(0, 96), slice(0, 2))
-        round_w1(3, nc.scalar.copy, slice(96, P), slice(0, 2))
-        round_w1(3, nc.vector.tensor_copy, slice(0, 56), slice(2, 4))
-        round_w1(3, nc.scalar.copy, slice(56, P), slice(2, 4))
+        share(2, 56)
+        share(3, 96, slice(0, 2))
+        share(3, 0, slice(2, 4))
         quantise_w1(1, 0, 2)
-        quantise_w1(1, 2, 4)
-        nc.vector.tensor_copy(x_codes1[:], x_all[1][:].indirect(offsets[:]))
+        for first, count in ((0, CHUNK), (CHUNK, CHUNK), (HALF, HALF)):
+            nc.vector.tensor_copy(x_codes1[:, first : first + count], x_all[1][:].indirect(entries(first, count)))
+        quantise_w1(1, 2, 4, tag="x_all1")
 
-        banks = {
-            (t, h): psum.tile([P, HALF], F32, name=f"first{t}{h}", tag=f"bank{2 * t + h}")
-            for t in range(PACK)
-            for h in range(2)
-        }
-
-        def first_product(z, t, h):
-            rows = slice(t * P, (t + 1) * P)
-            cols = slice(h * HALF, (h + 1) * HALF)
-            nc.tensor.matmul_mx(
-                out=banks[t, h][:],
-                lhsT=w1_codes[z][:, rows].bitcast(FP8X4),
-                lhsT_scale=w1_planes[z][:, rows],
-                rhs=(x_codes0 if z == 0 else x_codes1)[:, cols].bitcast(FP8X4),
-                rhs_scale=x_planes[4 * z : P, cols],
-                start=(z == 0),
-                stop=(z == PASSES - 1),
-            )
-
-        product = {t: sbuf(f"product{t}", [P, S], F32) for t in range(1, PACK)}
+        units = [(0, 0, CHUNK), (0, CHUNK, CHUNK), (1, 0, HALF), (0, HALF, HALF), (1, HALF, HALF), (2, 0, S), (3, 0, S)]
+        banks = [psum.tile([P, count], F32, name=f"first{g}", tag=f"bank{g}") for g, (t, first, count) in enumerate(units)]
+        product = [sbuf(f"product{t}", [P, S], F32) for t in range(PACK)]
         for z in range(PASSES):
-            for pair in range(2):
-                for h in range(2):
-                    for t in (2 * pair, 2 * pair + 1):
-                        first_product(z, t, h)
-                        if z == PASSES - 1 and t > 0:
-                            nc.scalar.copy(product[t][:, h * HALF : (h + 1) * HALF], banks[t, h][:])
+            for g, (t, first, count) in enumerate(units):
+                cols = slice(first, first + count)
+                nc.tensor.matmul_mx(
+                    out=banks[g][:],
+                    lhsT=w1_codes[z, t].bitcast(FP8X4),
+                    lhsT_scale=w1_planes[z, t],
+                    rhs=(x_codes0 if z == 0 else x_codes1)[:, cols].bitcast(FP8X4),
+                    rhs_scale=x_planes[4 * z : P, cols],
+                    start=(z == 0),
+                    stop=(z == PASSES - 1),
+                )
+                if z == PASSES - 1:
+                    nc.scalar.copy(product[t][:, cols], banks[g][:])
 
-        hidden_low = sbuf("hidden_low", [P, 2, S], F32)
-        h_grouped = [sbuf(f"h_grouped{c}", [P, PACK * CHUNK], BF16) for c in range(CHUNKS)]
+        hidden_low = [sbuf(f"hidden_low{h}", [P, 2, HALF], F32) for h in range(2)]
+        freed = ("x_all1", "w1_plane12", "x_codes1", "x_planes")
+        h_grouped = [sbuf(f"h_grouped{c}", [P, PACK * CHUNK], BF16, tag=freed[c]) for c in range(CHUNKS)]
 
         def add_position(target, t, first, count):
             nc.vector.tensor_tensor(
@@ -151,16 +144,12 @@ def tile_picked_posadd_none_p_kernel(
             dst = h_grouped[c][:].rearrange("p (g i t) -> p g t i", i=2, t=PACK)
             copy(dst[:, :, 2 * u : 2 * u + 2, :], pair.rearrange("p t (g i) -> p g t i", i=2))
 
-        picked = sbuf("picked", [P, S], F32)
-        for h in range(2):
-            nc.vector.tensor_copy(picked[:, h * HALF : (h + 1) * HALF], pe_all[0][:].indirect(entries(h * HALF, HALF)))
-        for h in range(2):
-            cols = slice(h * HALF, (h + 1) * HALF)
-            nc.vector.tensor_tensor(hidden_low[:, 0, cols], banks[0, h][:], picked[:, cols], ADD)
-        for h in range(2):
-            add_position(hidden_low[:, 1, h * HALF : (h + 1) * HALF], 1, h * HALF, HALF)
-            for c in (2 * h, 2 * h + 1):
-                round_pair(nc.scalar.copy, 0, c, hidden_low[:, :, c * CHUNK : (c + 1) * CHUNK])
+        for t, first, count in units[:5]:
+            low = hidden_low[first // HALF]
+            add_position(low[:, t, first % HALF : first % HALF + count], t, first, count)
+            if t == 1:
+                for i in range(2):
+                    round_pair(nc.scalar.copy, 0, first // CHUNK + i, low[:, :, i * CHUNK : (i + 1) * CHUNK])
         out_rows = out.rearrange("(b p) s -> p b s", p=P)
         ring = CHUNKS - 1
         hidden_high = sbuf("hidden_high", [P, 2, ring * CHUNK], F32)

@@ -115,7 +115,10 @@ def tile_picked_posadd_none_p_kernel(
 
         units = [(0, 0, CHUNK), (0, CHUNK, CHUNK), (1, 0, HALF), (0, HALF, HALF), (1, HALF, HALF), (2, 0, S), (3, 0, S)]
         banks = [psum.tile([P, count], F32, name=f"first{g}", tag=f"bank{g}") for g, (t, first, count) in enumerate(units)]
-        product = [sbuf(f"product{t}", [P, S], F32) for t in range(PACK)]
+        ring = CHUNKS - 1
+        late = sbuf("late", [P, 4 * ring * CHUNK], F32)
+        product = [sbuf(f"product{t}", [P, S], F32)[:] for t in range(PACK - 1)]
+        product.append(late[:, 2 * ring * CHUNK : 2 * ring * CHUNK + S])
         for z in range(PASSES):
             for g, (t, first, count) in enumerate(units):
                 cols = slice(first, first + count)
@@ -151,19 +154,19 @@ def tile_picked_posadd_none_p_kernel(
                 for i in range(2):
                     round_pair(nc.scalar.copy, 0, first // CHUNK + i, low[:, :, i * CHUNK : (i + 1) * CHUNK])
         out_rows = out.rearrange("(b p) s -> p b s", p=P)
-        ring = CHUNKS - 1
-        hidden_high = sbuf("hidden_high", [P, 2, ring * CHUNK], F32)
+        hidden_high = late[:, : 2 * ring * CHUNK].rearrange("p (t s) -> p t s", t=2)
         add_position(hidden_high[:, 0, :], 2, 0, ring * CHUNK)
         for c in range(ring):
             cols = slice(c * CHUNK, (c + 1) * CHUNK)
             add_position(hidden_high[:, 1, cols], 3, c * CHUNK, CHUNK)
             round_pair(nc.scalar.copy, 1, c, hidden_high[:, :, cols])
+        add_position(product[3][:, :CHUNK], 2, ring * CHUNK, CHUNK)
         for c in range(CHUNKS):
             if c == 1:
-                add_position(hidden_high[:, 0, :CHUNK], 2, ring * CHUNK, CHUNK)
-                add_position(hidden_high[:, 1, :CHUNK], 3, ring * CHUNK, CHUNK)
+                add_position(late[:, :CHUNK], 3, ring * CHUNK, CHUNK)
             if c == 2:
-                round_pair(nc.vector.tensor_copy, 1, ring, hidden_high[:, :, :CHUNK])
+                last = late[:].rearrange("p (t s) -> p t s", t=2)
+                round_pair(nc.vector.tensor_copy, 1, ring, last[:, ::-1, :CHUNK])
             cols = slice(c * CHUNK, (c + 1) * CHUNK)
             h_codes = sbuf(f"h_codes{c}", [P, CHUNK], U32)
             h_plane = sbuf(f"h_plane{c}", [P, CHUNK], U8)

@@ -135,45 +135,45 @@ def tile_picked_posadd_none_p_kernel(
                     nc.scalar.copy(product[t][:, cols], banks[g][:])
 
         hidden_low = [sbuf(f"hidden_low{h}", [P, 2, HALF], F32) for h in range(2)]
-        freed = ("x_all1", "w1_plane12", "x_codes1", "x_planes")
-        h_grouped = [sbuf(f"h_grouped{c}", [P, PACK * CHUNK], BF16, tag=freed[c]) for c in range(CHUNKS)]
+        freed = ("x_all1", "x_codes1")
+        h_halves = [sbuf(f"h_grouped{h}", [P, PACK * HALF], BF16, tag=freed[h]) for h in range(2)]
+        h_grouped = [h_halves[c // 2][:, (c % 2) * PACK * CHUNK : (c % 2 + 1) * PACK * CHUNK] for c in range(CHUNKS)]
 
         def add_position(target, t, first, count):
             nc.vector.tensor_tensor(
                 target, pe_all[t][:].indirect(entries(first, count)), product[t][:, first : first + count], ADD
             )
 
-        def round_pair(copy, u, c, pair):
-            dst = h_grouped[c][:].rearrange("p (g i t) -> p g t i", i=2, t=PACK)
+        def round_pair(copy, u, target, pair):
+            dst = target.rearrange("p (g i t) -> p g t i", i=2, t=PACK)
             copy(dst[:, :, 2 * u : 2 * u + 2, :], pair.rearrange("p t (g i) -> p g t i", i=2))
 
         for t, first, count in units[:5]:
             low = hidden_low[first // HALF]
             add_position(low[:, t, first % HALF : first % HALF + count], t, first, count)
             if t == 1:
-                for i in range(2):
-                    round_pair(nc.scalar.copy, 0, first // CHUNK + i, low[:, :, i * CHUNK : (i + 1) * CHUNK])
+                round_pair(nc.scalar.copy, 0, h_halves[first // HALF][:], low[:])
         out_rows = out.rearrange("(b p) s -> p b s", p=P)
         hidden_high = late[:, : 2 * ring * CHUNK].rearrange("p (t s) -> p t s", t=2)
         add_position(hidden_high[:, 0, :], 2, 0, ring * CHUNK)
         for c in range(ring):
             cols = slice(c * CHUNK, (c + 1) * CHUNK)
             add_position(hidden_high[:, 1, cols], 3, c * CHUNK, CHUNK)
-            round_pair(nc.scalar.copy, 1, c, hidden_high[:, :, cols])
+            round_pair(nc.scalar.copy, 1, h_grouped[c], hidden_high[:, :, cols])
         add_position(product[3][:, :CHUNK], 2, ring * CHUNK, CHUNK)
         for c in range(CHUNKS):
             if c == 1:
                 add_position(late[:, :CHUNK], 3, ring * CHUNK, CHUNK)
             if c == 2:
                 last = late[:].rearrange("p (t s) -> p t s", t=2)
-                round_pair(nc.vector.tensor_copy, 1, ring, last[:, ::-1, :CHUNK])
+                round_pair(nc.vector.tensor_copy, 1, h_grouped[ring], last[:, ::-1, :CHUNK])
             cols = slice(c * CHUNK, (c + 1) * CHUNK)
             h_codes = sbuf(f"h_codes{c}", [P, CHUNK], U32)
             h_plane = sbuf(f"h_plane{c}", [P, CHUNK], U8)
             nc.vector.quantize_mx(
                 out=h_codes[:].bitcast(FP8X4),
                 scales=h_plane[:],
-                in_=h_grouped[c][:],
+                in_=h_grouped[c],
             )
 
             def second_product(target, b):
@@ -188,16 +188,9 @@ def tile_picked_posadd_none_p_kernel(
                 )
 
             result = sbuf(f"result{c}", [P, 2, CHUNK], F32)
-            if c < CHUNKS - 2:
-                bank = psum.tile([P, 2, CHUNK], F32, name=f"second{c}", tag=f"bank{c}")
-                for b in range(2):
-                    second_product(bank[:, b, :], b)
-                nc.scalar.copy(result[:], bank[:])
-                nc.sync.dma_start(out_rows[:, :, cols], result[:])
-            else:
-                for b, copy in enumerate((nc.vector.tensor_copy, nc.scalar.copy)):
-                    tag = ((2, 3), (4, 5))[c - 2][b]
-                    bank = psum.tile([P, CHUNK], F32, name=f"second{c}{b}", tag=f"bank{tag}")
-                    second_product(bank[:], b)
-                    copy(result[:, b, :], bank[:])
-                nc.sync.dma_start(out_rows[:, :, cols], result[:])
+            first_copy = nc.scalar.copy if c < CHUNKS - 2 else nc.vector.tensor_copy
+            for b, copy in enumerate((first_copy, nc.scalar.copy)):
+                bank = psum.tile([P, CHUNK], F32, name=f"second{c}{b}", tag=f"bank{2 * c + b}")
+                second_product(bank[:], b)
+                copy(result[:, b, :], bank[:])
+            nc.sync.dma_start(out_rows[:, :, cols], result[:])

@@ -13,6 +13,7 @@ U16 = mybir.dt.uint16
 U8 = mybir.dt.uint8
 FP8X4 = mybir.dt.float8_e4m3fn_x4
 ADD = mybir.AluOpType.add
+COPY = mybir.ActivationFunctionType.Copy
 
 P = 128
 PACK = 4
@@ -46,24 +47,22 @@ def tile_picked_posadd_none_p_kernel(
         pe_rows = pe.rearrange("(p t) c -> p t c", t=PACK)
         w1_rows = w1.rearrange("(z p j) c -> z p j c", p=P, j=PACK)
         x_all = [sbuf(f"x_all{z}", [P, T], U32) for z in range(PASSES)]
-        pieces = [(0, 0, 2), (0, 2, 4), (1, 0, 2), (1, 2, 4)]
-        w1_raw = [sbuf(f"w1_raw{i}", [P, j1 - j0, H], F32) for i, (z, j0, j1) in enumerate(pieces)]
+        w1_raw = [sbuf(f"w1_raw{z}", [P, PACK, H], F32) for z in range(PASSES)]
         pe_all = [sbuf(f"pe_all{t}", [P, T], F32) for t in range(PACK)]
         w2_codes = sbuf("w2_codes", [P, N], U32)
 
         def load_words(tile, words):
             nc.sync.dma_start(tile[:].bitcast(I32), words.rearrange("p n r -> p (n r)").bitcast(I32))
 
-        load_words(x_all[0], x_words[0])
+        nc.sync.dma_start(w1_raw[0][:], w1_rows[0])
         nc.sync.dma_start(offsets[:], offs)
-        for i, (z, j0, j1) in enumerate(pieces):
-            nc.sync.dma_start(w1_raw[i][:], w1_rows[z, :, j0:j1, :])
-            if i == 0:
-                for q in range(4):
-                    nc.sync.dma_start(
-                        x_scale_rows[32 * q : 32 * q + 8, :].bitcast(I32),
-                        x_scales[:, 4 * q : 4 * q + 4, :].bitcast(I32),
-                    )
+        for q in range(4):
+            nc.sync.dma_start(
+                x_scale_rows[32 * q : 32 * q + 8, :].bitcast(I32),
+                x_scales[:, 4 * q : 4 * q + 4, :].bitcast(I32),
+            )
+        load_words(x_all[0], x_words[0])
+        nc.sync.dma_start(w1_raw[1][:], w1_rows[1])
         load_words(x_all[1], x_words[1])
         for t in range(PACK):
             nc.sync.dma_start(pe_all[t][:], pe_rows[:, t, :])
@@ -74,111 +73,99 @@ def tile_picked_posadd_none_p_kernel(
             )
 
         x_planes = sbuf("x_planes", [P, S], U8)
-        x_codes0 = sbuf("x_codes0", [P, S], U32)
-        x_codes1 = sbuf("x_codes1", [P, S], U32)
-        nc.vector.tensor_copy(x_codes0[:], x_all[0][:].indirect(offsets[:]))
-        nc.vector.tensor_copy(x_planes[:], x_scale_rows[:].indirect(offsets[:]))
+        x_codes = [sbuf(f"x_codes{z}", [P, S], U32) for z in range(PASSES)]
 
         w1_grouped = [sbuf(f"w1_grouped{z}", [P, PACK * H], BF16) for z in range(PASSES)]
-        w1_codes, w1_planes = {}, {}
+        w1_codes = {}
+        w1_planes = [sbuf(f"w1_plane{z}", [P, H], U8) for z in range(PASSES)]
 
-        def round_w1(i, copy, columns, planes):
-            z, j0, j1 = pieces[i]
-            dst = w1_grouped[z][:].rearrange("p (t m j) -> p m t j", t=PACK, j=PACK)[:, columns, planes, j0:j1]
-            copy(dst, w1_raw[i][:].rearrange("p j (m t) -> p m t j", t=PACK)[:, columns, planes, :])
+        def round_w1(z, copy, columns):
+            dst = w1_grouped[z][:].rearrange("p (t m j) -> p m t j", t=PACK, j=PACK)[:, columns, :, :]
+            copy(dst, w1_raw[z][:].rearrange("p j (m t) -> p m t j", t=PACK)[:, columns, :, :])
 
-        def quantise_w1(z, t0, t1, tag=None):
-            codes = sbuf(f"w1_codes{z}{t0}", [P, (t1 - t0) * P], U32, tag=tag)
-            plane = sbuf(f"w1_plane{z}{t0}", [P, (t1 - t0) * P], U8)
-            nc.vector.quantize_mx(out=codes[:].bitcast(FP8X4), scales=plane[:], in_=w1_grouped[z][:, t0 * H : t1 * H])
-            for t in range(t0, t1):
-                w1_codes[z, t] = codes[:, (t - t0) * P : (t - t0 + 1) * P]
-                w1_planes[z, t] = plane[:, (t - t0) * P : (t - t0 + 1) * P]
+        def quantise_w1(z, tag=None):
+            w1_codes[z] = sbuf(f"w1_codes{z}", [P, H], U32, tag=tag)
+            nc.vector.quantize_mx(out=w1_codes[z][:].bitcast(FP8X4), scales=w1_planes[z][:], in_=w1_grouped[z][:])
 
-        every = slice(None)
+        round_w1(0, nc.scalar.copy, slice(0, P))
+        nc.vector.tensor_copy(x_planes[:], x_scale_rows[:].indirect(offsets[:]))
+        nc.vector.tensor_copy(x_codes[0][:], x_all[0][:].indirect(offsets[:]))
+        quantise_w1(0, tag="x_all0")
+        round_w1(1, nc.vector.tensor_copy, slice(0, 76))
+        round_w1(1, nc.scalar.copy, slice(76, P))
+        quantise_w1(1)
+        for h in range(2):
+            nc.vector.tensor_copy(x_codes[1][:, h * HALF : (h + 1) * HALF], x_all[1][:].indirect(entries(h * HALF, HALF)))
+        last = S - CHUNK
 
-        def share(i, columns, planes=every):
-            if columns > 0:
-                round_w1(i, nc.vector.tensor_copy, slice(0, columns), planes)
-            round_w1(i, nc.scalar.copy, slice(columns, P), planes)
-
-        share(0, 32)
-        share(1, 64)
-        quantise_w1(0, 0, 4)
-        share(2, 56)
-        share(3, 96, slice(0, 2))
-        share(3, 0, slice(2, 4))
-        quantise_w1(1, 0, 2)
-        for first, count in ((0, CHUNK), (CHUNK, CHUNK), (HALF, HALF)):
-            nc.vector.tensor_copy(x_codes1[:, first : first + count], x_all[1][:].indirect(entries(first, count)))
-        quantise_w1(1, 2, 4, tag="x_all1")
-
-        units = [(0, 0, CHUNK), (0, CHUNK, CHUNK), (1, 0, HALF), (0, HALF, HALF), (1, HALF, HALF), (2, 0, S), (3, 0, S)]
-        banks = [psum.tile([P, count], F32, name=f"first{g}", tag=f"bank{g}") for g, (t, first, count) in enumerate(units)]
-        ring = CHUNKS - 1
-        late = sbuf("late", [P, 4 * ring * CHUNK], F32)
-        product = [sbuf(f"product{t}", [P, S], F32)[:] for t in range(PACK - 1)]
-        product.append(late[:, 2 * ring * CHUNK : 2 * ring * CHUNK + S])
+        units = [(0, 2, 0, HALF), (0, 2, last, CHUNK), (2, PACK, last, CHUNK), (2, PACK, 0, HALF), (0, PACK, HALF, CHUNK)]
+        banks = [
+            psum.tile([P, t1 - t0, count], F32, name=f"first{g}", tag=f"bank{g}")
+            for g, (t0, t1, first, count) in enumerate(units)
+        ]
         for z in range(PASSES):
-            for g, (t, first, count) in enumerate(units):
+            for g, (t0, t1, first, count) in enumerate(units):
                 cols = slice(first, first + count)
-                nc.tensor.matmul_mx(
-                    out=banks[g][:],
-                    lhsT=w1_codes[z, t].bitcast(FP8X4),
-                    lhsT_scale=w1_planes[z, t],
-                    rhs=(x_codes0 if z == 0 else x_codes1)[:, cols].bitcast(FP8X4),
-                    rhs_scale=x_planes[4 * z : P, cols],
-                    start=(z == 0),
-                    stop=(z == PASSES - 1),
-                )
-                if z == PASSES - 1:
-                    nc.scalar.copy(product[t][:, cols], banks[g][:])
+                for t in range(t0, t1):
+                    rows = slice(t * P, (t + 1) * P)
+                    nc.tensor.matmul_mx(
+                        out=banks[g][:, t - t0, :],
+                        lhsT=w1_codes[z][:, rows].bitcast(FP8X4),
+                        lhsT_scale=w1_planes[z][:, rows],
+                        rhs=x_codes[z][:, cols].bitcast(FP8X4),
+                        rhs_scale=x_planes[4 * z : P, cols],
+                        start=(z == 0 and t == t0),
+                        stop=(z == PASSES - 1 and t == t1 - 1),
+                    )
 
-        hidden_low = [sbuf(f"hidden_low{h}", [P, 2, HALF], F32) for h in range(2)]
-        freed = ("x_all1", "x_codes1")
-        h_halves = [sbuf(f"h_grouped{h}", [P, PACK * HALF], BF16, tag=freed[h]) for h in range(2)]
-        h_grouped = [h_halves[c // 2][:, (c % 2) * PACK * CHUNK : (c % 2 + 1) * PACK * CHUNK] for c in range(CHUNKS)]
+        picked = sbuf("picked", [P, PACK * S], F32)[:].rearrange("p (t s) -> p t s", t=PACK)
+        h_grouped = sbuf("h_grouped", [P, PACK * S], BF16)
+        hidden = sbuf("hidden", [P, 2 * CHUNK], F32)[:].rearrange("p (t s) -> p t s", s=CHUNK)
 
-        def add_position(target, t, first, count):
+        def window(t, first, count):
+            return pe_all[t][:].indirect(entries(first, count))
+
+        def pick(t, first, count):
+            nc.scalar.activation(picked[:, t, first : first + count], window(t, first, count), COPY)
+
+        def pick_and_add(t):
+            nc.vector.tensor_tensor(hidden[:, t - 2, :], window(t, last, CHUNK), emptied[:, t - 2, :], ADD)
+
+        def add_planes(g, first, count):
+            t0, t1, start = units[g][:3]
+            cols = slice(first, first + count)
             nc.vector.tensor_tensor(
-                target, pe_all[t][:].indirect(entries(first, count)), product[t][:, first : first + count], ADD
+                h_grouped[:].rearrange("p (s t) -> p s t", t=PACK)[:, cols, t0:t1],
+                banks[g][:, :, first - start : first - start + count].rearrange("p t s -> p s t"),
+                picked[:, t0:t1, cols].rearrange("p t s -> p s t"),
+                ADD,
             )
 
-        def round_pair(copy, u, target, pair):
-            dst = target.rearrange("p (g i t) -> p g t i", i=2, t=PACK)
-            copy(dst[:, :, 2 * u : 2 * u + 2, :], pair.rearrange("p t (g i) -> p g t i", i=2))
+        pick(0, 0, S)
+        pick(1, 0, HALF)
+        nc.vector.tensor_copy(picked[:, 1, HALF:], window(1, HALF, HALF))
+        emptied = sbuf("emptied", [P, 2, CHUNK], F32, tag="pe_all1")
+        nc.scalar.copy(emptied[:], banks[2][:])
+        add_planes(0, 0, HALF)
+        add_planes(1, last, CHUNK)
+        pick_and_add(2)
+        pick(2, 0, last)
 
-        for t, first, count in units[:5]:
-            low = hidden_low[first // HALF]
-            add_position(low[:, t, first % HALF : first % HALF + count], t, first, count)
-            if t == 1:
-                round_pair(nc.scalar.copy, 0, h_halves[first // HALF][:], low[:])
         out_rows = out.rearrange("(b p) s -> p b s", p=P)
-        hidden_high = late[:, : 2 * ring * CHUNK].rearrange("p (t s) -> p t s", t=2)
-        add_position(hidden_high[:, 0, :], 2, 0, ring * CHUNK)
-        for c in range(ring):
-            cols = slice(c * CHUNK, (c + 1) * CHUNK)
-            add_position(hidden_high[:, 1, cols], 3, c * CHUNK, CHUNK)
-            round_pair(nc.scalar.copy, 1, h_grouped[c], hidden_high[:, :, cols])
-        add_position(product[3][:, :CHUNK], 2, ring * CHUNK, CHUNK)
-        for c in range(CHUNKS):
-            if c == 1:
-                add_position(late[:, :CHUNK], 3, ring * CHUNK, CHUNK)
-            if c == 2:
-                last = late[:].rearrange("p (t s) -> p t s", t=2)
-                round_pair(nc.vector.tensor_copy, 1, h_grouped[ring], last[:, ::-1, :CHUNK])
-            cols = slice(c * CHUNK, (c + 1) * CHUNK)
+
+        def second_layer(c, tags, first_copy):
             h_codes = sbuf(f"h_codes{c}", [P, CHUNK], U32)
             h_plane = sbuf(f"h_plane{c}", [P, CHUNK], U8)
             nc.vector.quantize_mx(
                 out=h_codes[:].bitcast(FP8X4),
                 scales=h_plane[:],
-                in_=h_grouped[c],
+                in_=h_grouped[:, c * PACK * CHUNK : (c + 1) * PACK * CHUNK],
             )
-
-            def second_product(target, b):
+            result = sbuf(f"result{c}", [P, 2, CHUNK], F32)
+            for b, copy in enumerate((first_copy, nc.scalar.copy)):
+                bank = psum.tile([P, CHUNK], F32, name=f"second{c}{b}", tag=f"bank{tags[b]}")
                 nc.tensor.matmul_mx(
-                    out=target,
+                    out=bank[:],
                     lhsT=w2_codes[:, b * P : (b + 1) * P].bitcast(FP8X4),
                     lhsT_scale=w2_scale_rows[:, b * P : (b + 1) * P],
                     rhs=h_codes[:].bitcast(FP8X4),
@@ -186,11 +173,21 @@ def tile_picked_posadd_none_p_kernel(
                     start=True,
                     stop=True,
                 )
-
-            result = sbuf(f"result{c}", [P, 2, CHUNK], F32)
-            first_copy = nc.scalar.copy if c < CHUNKS - 2 else nc.vector.tensor_copy
-            for b, copy in enumerate((first_copy, nc.scalar.copy)):
-                bank = psum.tile([P, CHUNK], F32, name=f"second{c}{b}", tag=f"bank{2 * c + b}")
-                second_product(bank[:], b)
                 copy(result[:, b, :], bank[:])
-            nc.sync.dma_start(out_rows[:, :, cols], result[:])
+            nc.sync.dma_start(out_rows[:, :, c * CHUNK : (c + 1) * CHUNK], result[:])
+
+        pick_and_add(3)
+        pick(3, 0, CHUNK)
+        add_planes(3, 0, CHUNK)
+        pick(3, CHUNK, CHUNK)
+        add_planes(3, CHUNK, CHUNK)
+        nc.scalar.copy(
+            h_grouped[:, last * PACK :].rearrange("p (g i t) -> p g t i", i=2, t=PACK)[:, :, 2:, :],
+            hidden.rearrange("p t (g i) -> p g t i", i=2),
+        )
+        pick(3, HALF, CHUNK)
+        second_layer(0, (5, 6), nc.scalar.copy)
+        second_layer(3, (7, 0), nc.scalar.copy)
+        add_planes(4, HALF, CHUNK)
+        second_layer(1, (1, 2), nc.scalar.copy)
+        second_layer(2, (3, 5), nc.vector.tensor_copy)

@@ -1,3 +1,4 @@
+import itertools
 from contextlib import ExitStack
 
 import concourse.mybir as mybir
@@ -94,17 +95,19 @@ def tile_picked_posadd_none_p_kernel(
         round_w1(1, nc.vector.tensor_copy, slice(0, 76))
         round_w1(1, nc.scalar.copy, slice(76, P))
         quantise_w1(1)
-        for h in range(2):
+        for h in (1, 0):
             nc.vector.tensor_copy(x_codes[1][:, h * HALF : (h + 1) * HALF], x_all[1][:].indirect(entries(h * HALF, HALF)))
         last = S - CHUNK
 
         units = [(0, 2, 0, HALF), (0, 2, last, CHUNK), (2, PACK, last, CHUNK), (2, PACK, 0, HALF), (0, PACK, HALF, CHUNK)]
-        banks = [
-            psum.tile([P, t1 - t0, count], F32, name=f"first{g}", tag=f"bank{g}")
-            for g, (t0, t1, first, count) in enumerate(units)
-        ]
-        for z in range(PASSES):
-            for g, (t0, t1, first, count) in enumerate(units):
+        banks = {}
+
+        def first_product(group, tags):
+            for g, tag in zip(group, tags):
+                t0, t1, first, count = units[g]
+                banks[g] = psum.tile([P, t1 - t0, count], F32, name=f"first{g}", tag=f"bank{tag}")
+            for z, g in itertools.product(range(PASSES), group):
+                t0, t1, first, count = units[g]
                 cols = slice(first, first + count)
                 for t in range(t0, t1):
                     rows = slice(t * P, (t + 1) * P)
@@ -118,6 +121,7 @@ def tile_picked_posadd_none_p_kernel(
                         stop=(z == PASSES - 1 and t == t1 - 1),
                     )
 
+        first_product((2, 1, 0, 3), (2, 1, 0, 3))
         picked = sbuf("picked", [P, PACK * S], F32)[:].rearrange("p (t s) -> p t s", t=PACK)
         h_grouped = sbuf("h_grouped", [P, PACK * S], BF16)
         hidden = sbuf("hidden", [P, 2 * CHUNK], F32)[:].rearrange("p (t s) -> p t s", s=CHUNK)
@@ -148,6 +152,7 @@ def tile_picked_posadd_none_p_kernel(
         nc.scalar.copy(emptied[:], banks[2][:])
         add_planes(0, 0, HALF)
         add_planes(1, last, CHUNK)
+        first_product([4], [1])
         pick_and_add(2)
         pick(2, 0, last)
 
@@ -189,5 +194,5 @@ def tile_picked_posadd_none_p_kernel(
         second_layer(0, (5, 6), nc.scalar.copy)
         second_layer(3, (7, 0), nc.scalar.copy)
         add_planes(4, HALF, CHUNK)
-        second_layer(1, (1, 2), nc.scalar.copy)
+        second_layer(1, (4, 2), nc.scalar.copy)
         second_layer(2, (3, 5), nc.vector.tensor_copy)

@@ -139,9 +139,9 @@ def tile_picked_posadd_none_p_kernel(
             t0, t1, start = units[g][:3]
             cols = slice(first, first + count)
             nc.vector.tensor_tensor(
-                h_grouped[:].rearrange("p (s t) -> p s t", t=PACK)[:, cols, t0:t1],
-                banks[g][:, :, first - start : first - start + count].rearrange("p t s -> p s t"),
-                picked[:, t0:t1, cols].rearrange("p t s -> p s t"),
+                h_grouped[:, first * PACK : (first + count) * PACK].rearrange("p (g i t) -> p g t i", i=2, t=PACK)[:, :, t0:t1, :],
+                banks[g][:, :, first - start : first - start + count].rearrange("p t (g i) -> p g t i", i=2),
+                picked[:, t0:t1, cols].rearrange("p t (g i) -> p g t i", i=2),
                 ADD,
             )
 

@@ -194,5 +194,5 @@ def tile_picked_posadd_none_p_kernel(
         second_layer(0, (5, 6), nc.scalar.copy)
         second_layer(3, (7, 0), nc.scalar.copy)
         add_planes(4, HALF, CHUNK)
-        second_layer(1, (4, 2), nc.scalar.copy)
+        second_layer(1, (4, 2), nc.vector.tensor_copy)
         second_layer(2, (3, 5), nc.vector.tensor_copy)

@@ -158,7 +158,7 @@ def tile_picked_posadd_none_p_kernel(
 
         out_rows = out.rearrange("(b p) s -> p b s", p=P)
 
-        def second_layer(c, tags, first_copy):
+        def second_layer(c, tags, first_copy, stores=1):
             h_codes = sbuf(f"h_codes{c}", [P, CHUNK], U32)
             h_plane = sbuf(f"h_plane{c}", [P, CHUNK], U8)
             nc.vector.quantize_mx(
@@ -179,7 +179,9 @@ def tile_picked_posadd_none_p_kernel(
                     stop=True,
                 )
                 copy(result[:, b, :], bank[:])
-            nc.sync.dma_start(out_rows[:, :, c * CHUNK : (c + 1) * CHUNK], result[:])
+            for k in range(stores):
+                blocks = slice(k * 2 // stores, (k + 1) * 2 // stores)
+                nc.sync.dma_start(out_rows[:, blocks, c * CHUNK : (c + 1) * CHUNK], result[:, blocks, :])
 
         pick_and_add(3)
         pick(3, 0, CHUNK)
@@ -191,7 +193,7 @@ def tile_picked_posadd_none_p_kernel(
             hidden.rearrange("p t (g i) -> p g t i", i=2),
         )
         pick(3, HALF, CHUNK)
-        second_layer(0, (5, 6), nc.scalar.copy)
+        second_layer(0, (5, 6), nc.scalar.copy, stores=2)
         second_layer(3, (7, 0), nc.scalar.copy)
         add_planes(4, HALF, CHUNK)
         second_layer(1, (4, 2), nc.vector.tensor_copy)

@@ -95,7 +95,7 @@ def tile_picked_posadd_none_p_kernel(
         round_w1(1, nc.vector.tensor_copy, slice(0, 76))
         round_w1(1, nc.scalar.copy, slice(76, P))
         quantise_w1(1)
-        for h in (1, 0):
+        for h in range(2):
             nc.vector.tensor_copy(x_codes[1][:, h * HALF : (h + 1) * HALF], x_all[1][:].indirect(entries(h * HALF, HALF)))
         last = S - CHUNK
 
@@ -121,7 +121,7 @@ def tile_picked_posadd_none_p_kernel(
                         stop=(z == PASSES - 1 and t == t1 - 1),
                     )
 
-        first_product((2, 1, 0, 3), (2, 1, 0, 3))
+        first_product((0, 2, 1, 3), (0, 2, 1, 3))
         picked = sbuf("picked", [P, PACK * S], F32)[:].rearrange("p (t s) -> p t s", t=PACK)
         h_grouped = sbuf("h_grouped", [P, PACK * S], BF16)
         hidden = sbuf("hidden", [P, 2 * CHUNK], F32)[:].rearrange("p (t s) -> p t s", s=CHUNK)

@@ -1,4 +1,3 @@
-import itertools
 from contextlib import ExitStack
 
 import concourse.mybir as mybir
@@ -21,7 +20,6 @@ PACK = 4
 PASSES = K // (P * PACK)
 HALF = S // 2
 CHUNK = 128
-CHUNKS = S // CHUNK
 LIST_ROWS = 16
 
 
@@ -75,7 +73,6 @@ def tile_picked_posadd_none_p_kernel(
 
         x_planes = sbuf("x_planes", [P, S], U8)
         x_codes = [sbuf(f"x_codes{z}", [P, S], U32) for z in range(PASSES)]
-
         w1_grouped = [sbuf(f"w1_grouped{z}", [P, PACK * H], BF16) for z in range(PASSES)]
         w1_codes = {}
         w1_planes = [sbuf(f"w1_plane{z}", [P, H], U8) for z in range(PASSES)]
@@ -95,36 +92,40 @@ def tile_picked_posadd_none_p_kernel(
         round_w1(1, nc.vector.tensor_copy, slice(0, 76))
         round_w1(1, nc.scalar.copy, slice(76, P))
         quantise_w1(1)
-        for h in range(2):
-            nc.vector.tensor_copy(x_codes[1][:, h * HALF : (h + 1) * HALF], x_all[1][:].indirect(entries(h * HALF, HALF)))
+        for first in (0, HALF):
+            nc.vector.tensor_copy(x_codes[1][:, first : first + HALF], x_all[1][:].indirect(entries(first, HALF)))
         last = S - CHUNK
 
-        units = [(0, 2, 0, HALF), (0, 2, last, CHUNK), (2, PACK, last, CHUNK), (2, PACK, 0, HALF), (0, PACK, HALF, CHUNK)]
-        banks = {}
+        def product_bank(name, count, tag):
+            return psum.tile([P, 2, count], F32, name=name, tag=tag)
 
-        def first_product(group, tags):
-            for g, tag in zip(group, tags):
-                t0, t1, first, count = units[g]
-                banks[g] = psum.tile([P, t1 - t0, count], F32, name=f"first{g}", tag=f"bank{tag}")
-            for z, g in itertools.product(range(PASSES), group):
-                t0, t1, first, count = units[g]
-                cols = slice(first, first + count)
-                for t in range(t0, t1):
-                    rows = slice(t * P, (t + 1) * P)
-                    nc.tensor.matmul_mx(
-                        out=banks[g][:, t - t0, :],
-                        lhsT=w1_codes[z][:, rows].bitcast(FP8X4),
-                        lhsT_scale=w1_planes[z][:, rows],
-                        rhs=x_codes[z][:, cols].bitcast(FP8X4),
-                        rhs_scale=x_planes[4 * z : P, cols],
-                        start=(z == 0 and t == t0),
-                        stop=(z == PASSES - 1 and t == t1 - 1),
-                    )
+        def product_pass(z, bank, t0, first, count):
+            cols = slice(first, first + count)
+            for slot in range(2):
+                rows = slice((t0 + slot) * P, (t0 + slot + 1) * P)
+                nc.tensor.matmul_mx(
+                    out=bank[:, slot, :],
+                    lhsT=w1_codes[z][:, rows].bitcast(FP8X4),
+                    lhsT_scale=w1_planes[z][:, rows],
+                    rhs=x_codes[z][:, cols].bitcast(FP8X4),
+                    rhs_scale=x_planes[4 * z : P, cols],
+                    start=(z == 0 and slot == 0),
+                    stop=(z == PASSES - 1 and slot == 1),
+                )
 
-        first_product((0, 2, 1, 3), (0, 2, 1, 3))
+        low01 = product_bank("low01", HALF, "bank0")
+        last23 = product_bank("last23", CHUNK, "bank1")
+        high01 = product_bank("high01", HALF, "bank2")
+        first23 = product_bank("first23", CHUNK, "bank3")
+        early = [(low01, 0, 0, HALF), (last23, 2, last, CHUNK), (high01, 0, HALF, HALF), (first23, 2, 0, CHUNK)]
+        for z in range(PASSES):
+            for unit in early:
+                product_pass(z, *unit)
+
         picked = sbuf("picked", [P, PACK * S], F32)[:].rearrange("p (t s) -> p t s", t=PACK)
+        hidden = sbuf("hidden", [P, PACK * CHUNK], F32)[:].rearrange("p (t s) -> p t s", t=PACK)
+        pairs = sbuf("pairs", [P, 2 * 2 * CHUNK], BF16)
         h_grouped = sbuf("h_grouped", [P, PACK * S], BF16)
-        hidden = sbuf("hidden", [P, 2 * CHUNK], F32)[:].rearrange("p (t s) -> p t s", s=CHUNK)
 
         def window(t, first, count):
             return pe_all[t][:].indirect(entries(first, count))
@@ -133,26 +134,48 @@ def tile_picked_posadd_none_p_kernel(
             nc.scalar.activation(picked[:, t, first : first + count], window(t, first, count), COPY)
 
         def pick_and_add(t):
-            nc.vector.tensor_tensor(hidden[:, t - 2, :], window(t, last, CHUNK), emptied[:, t - 2, :], ADD)
+            nc.vector.tensor_tensor(hidden[:, t, :], window(t, last, CHUNK), emptied[:, t - 2, :], ADD)
 
-        def add_planes(g, first, count):
-            t0, t1, start = units[g][:3]
-            cols = slice(first, first + count)
+        def by_twos(planes):
+            return planes.rearrange("p t (g i) -> p g t i", i=2)
+
+        def lines(c):
+            return h_grouped[:, c * PACK * CHUNK : (c + 1) * PACK * CHUNK]
+
+        def add_pair(dst, bank, start, t0, c):
+            first = c * CHUNK
             nc.vector.tensor_tensor(
-                h_grouped[:, first * PACK : (first + count) * PACK].rearrange("p (g i t) -> p g t i", i=2, t=PACK)[:, :, t0:t1, :],
-                banks[g][:, :, first - start : first - start + count].rearrange("p t (g i) -> p g t i", i=2),
-                picked[:, t0:t1, cols].rearrange("p t (g i) -> p g t i", i=2),
+                dst,
+                by_twos(bank[:, :, first - start : first - start + CHUNK]),
+                by_twos(picked[:, t0 : t0 + 2, first : first + CHUNK]),
                 ADD,
             )
 
+        def add_in_place(bank, start, t0, c):
+            add_pair(lines(c).rearrange("p (g i t) -> p g t i", i=2, t=PACK)[:, :, t0 : t0 + 2, :], bank, start, t0, c)
+
+        def add_as_words(bank, start, t0, c):
+            add_pair(pairs[:, t0 * CHUNK : (t0 + 2) * CHUNK].rearrange("p (g i t) -> p g t i", i=2, t=2), bank, start, t0, c)
+
+        def weave(c):
+            nc.scalar.copy(
+                lines(c).bitcast(U32).rearrange("p (s w) -> p s w", w=2),
+                pairs[:].bitcast(U32).rearrange("p (w s) -> p s w", w=2),
+            )
+
         pick(0, 0, S)
-        pick(1, 0, HALF)
+        pick(1, 0, CHUNK)
+        pick(1, CHUNK, CHUNK)
         nc.vector.tensor_copy(picked[:, 1, HALF:], window(1, HALF, HALF))
         emptied = sbuf("emptied", [P, 2, CHUNK], F32, tag="pe_all1")
-        nc.scalar.copy(emptied[:], banks[2][:])
-        add_planes(0, 0, HALF)
-        add_planes(1, last, CHUNK)
-        first_product([4], [1])
+        nc.scalar.copy(emptied[:], last23[:])
+        add_in_place(low01, 0, 0, 0)
+        add_as_words(low01, 0, 0, 1)
+        middle23 = product_bank("middle23", HALF, "bank0")
+        for z in range(PASSES):
+            product_pass(z, middle23, 2, CHUNK, HALF)
+        nc.vector.tensor_tensor(hidden[:, 0:2, :], high01[:, :, CHUNK:], picked[:, 0:2, last:], ADD)
+        add_in_place(high01, HALF, 0, 2)
         pick_and_add(2)
         pick(2, 0, last)
 
@@ -185,16 +208,14 @@ def tile_picked_posadd_none_p_kernel(
 
         pick_and_add(3)
         pick(3, 0, CHUNK)
-        add_planes(3, 0, CHUNK)
         pick(3, CHUNK, CHUNK)
-        add_planes(3, CHUNK, CHUNK)
-        nc.scalar.copy(
-            h_grouped[:, last * PACK :].rearrange("p (g i t) -> p g t i", i=2, t=PACK)[:, :, 2:, :],
-            hidden.rearrange("p t (g i) -> p g t i", i=2),
-        )
+        add_in_place(first23, 0, 2, 0)
+        nc.scalar.copy(lines(3).rearrange("p (g i t) -> p g t i", i=2, t=PACK), by_twos(hidden))
         pick(3, HALF, CHUNK)
-        second_layer(0, (5, 6), nc.scalar.copy, stores=2)
-        second_layer(3, (7, 0), nc.scalar.copy)
-        add_planes(4, HALF, CHUNK)
-        second_layer(1, (4, 2), nc.vector.tensor_copy)
-        second_layer(2, (3, 5), nc.vector.tensor_copy)
+        add_as_words(middle23, CHUNK, 2, 1)
+        weave(1)
+        second_layer(0, (4, 5), nc.scalar.copy, stores=2)
+        second_layer(3, (6, 7), nc.scalar.copy)
+        add_in_place(middle23, CHUNK, 2, 2)
+        second_layer(1, (1, 2), nc.vector.tensor_copy)
+        second_layer(2, (3, 4), nc.vector.tensor_copy)

@@ -96,12 +96,12 @@ def tile_picked_posadd_none_p_kernel(
             nc.vector.tensor_copy(x_codes[1][:, first : first + HALF], x_all[1][:].indirect(entries(first, HALF)))
         last = S - CHUNK
 
-        def product_bank(name, count, tag):
-            return psum.tile([P, 2, count], F32, name=name, tag=tag)
+        def product_bank(name, count, tag, phases=2):
+            return psum.tile([P, phases, count], F32, name=name, tag=tag)
 
-        def product_pass(z, bank, t0, first, count):
+        def product_pass(z, bank, t0, first, count, phases=2):
             cols = slice(first, first + count)
-            for slot in range(2):
+            for slot in range(phases):
                 rows = slice((t0 + slot) * P, (t0 + slot + 1) * P)
                 nc.tensor.matmul_mx(
                     out=bank[:, slot, :],
@@ -110,20 +110,20 @@ def tile_picked_posadd_none_p_kernel(
                     rhs=x_codes[z][:, cols].bitcast(FP8X4),
                     rhs_scale=x_planes[4 * z : P, cols],
                     start=(z == 0 and slot == 0),
-                    stop=(z == PASSES - 1 and slot == 1),
+                    stop=(z == PASSES - 1 and slot == phases - 1),
                 )
 
         low01 = product_bank("low01", HALF, "bank0")
         last23 = product_bank("last23", CHUNK, "bank1")
-        high01 = product_bank("high01", HALF, "bank2")
-        first23 = product_bank("first23", CHUNK, "bank3")
-        early = [(low01, 0, 0, HALF), (last23, 2, last, CHUNK), (high01, 0, HALF, HALF), (first23, 2, 0, CHUNK)]
+        last01 = product_bank("last01", CHUNK, "bank2")
+        low23 = product_bank("low23", HALF, "bank3")
+        early = [(low01, 0, 0, HALF), (last23, 2, last, CHUNK), (last01, 0, last, CHUNK), (low23, 2, 0, HALF)]
         for z in range(PASSES):
             for unit in early:
                 product_pass(z, *unit)
 
         picked = sbuf("picked", [P, PACK * S], F32)[:].rearrange("p (t s) -> p t s", t=PACK)
-        hidden = sbuf("hidden", [P, PACK * CHUNK], F32)[:].rearrange("p (t s) -> p t s", t=PACK)
+        hidden = sbuf("hidden", [P, 2 * CHUNK], F32)[:].rearrange("p (t s) -> p t s", t=2)
         pairs = sbuf("pairs", [P, 2 * 2 * CHUNK], BF16)
         h_grouped = sbuf("h_grouped", [P, PACK * S], BF16)
 
@@ -134,7 +134,7 @@ def tile_picked_posadd_none_p_kernel(
             nc.scalar.activation(picked[:, t, first : first + count], window(t, first, count), COPY)
 
         def pick_and_add(t):
-            nc.vector.tensor_tensor(hidden[:, t, :], window(t, last, CHUNK), emptied[:, t - 2, :], ADD)
+            nc.vector.tensor_tensor(hidden[:, t - 2, :], window(t, last, CHUNK), emptied[:, t - 2, :], ADD)
 
         def by_twos(planes):
             return planes.rearrange("p t (g i) -> p g t i", i=2)
@@ -142,20 +142,24 @@ def tile_picked_posadd_none_p_kernel(
         def lines(c):
             return h_grouped[:, c * PACK * CHUNK : (c + 1) * PACK * CHUNK]
 
-        def add_pair(dst, bank, start, t0, c):
+        def add_planes(dst, bank, start, t0, t1, c):
             first = c * CHUNK
             nc.vector.tensor_tensor(
                 dst,
                 by_twos(bank[:, :, first - start : first - start + CHUNK]),
-                by_twos(picked[:, t0 : t0 + 2, first : first + CHUNK]),
+                by_twos(picked[:, t0:t1, first : first + CHUNK]),
                 ADD,
             )
 
-        def add_in_place(bank, start, t0, c):
-            add_pair(lines(c).rearrange("p (g i t) -> p g t i", i=2, t=PACK)[:, :, t0 : t0 + 2, :], bank, start, t0, c)
+        def slots(c, t0, t1):
+            return lines(c).rearrange("p (g i t) -> p g t i", i=2, t=PACK)[:, :, t0:t1, :]
+
+        def add_in_place(bank, start, t0, t1, c):
+            add_planes(slots(c, t0, t1), bank, start, t0, t1, c)
 
         def add_as_words(bank, start, t0, c):
-            add_pair(pairs[:, t0 * CHUNK : (t0 + 2) * CHUNK].rearrange("p (g i t) -> p g t i", i=2, t=2), bank, start, t0, c)
+            words = pairs[:, t0 * CHUNK : (t0 + 2) * CHUNK].rearrange("p (g i t) -> p g t i", i=2, t=2)
+            add_planes(words, bank, start, t0, t0 + 2, c)
 
         def weave(c):
             nc.scalar.copy(
@@ -164,18 +168,16 @@ def tile_picked_posadd_none_p_kernel(
             )
 
         pick(0, 0, S)
-        pick(1, 0, CHUNK)
-        pick(1, CHUNK, CHUNK)
+        pick(1, 0, HALF)
         nc.vector.tensor_copy(picked[:, 1, HALF:], window(1, HALF, HALF))
         emptied = sbuf("emptied", [P, 2, CHUNK], F32, tag="pe_all1")
         nc.scalar.copy(emptied[:], last23[:])
-        add_in_place(low01, 0, 0, 0)
+        add_in_place(low01, 0, 0, 2, 0)
         add_as_words(low01, 0, 0, 1)
-        middle23 = product_bank("middle23", HALF, "bank0")
+        add_in_place(last01, last, 0, 2, 3)
+        third = product_bank("third", CHUNK, "bank2", PACK)
         for z in range(PASSES):
-            product_pass(z, middle23, 2, CHUNK, HALF)
-        nc.vector.tensor_tensor(hidden[:, 0:2, :], high01[:, :, CHUNK:], picked[:, 0:2, last:], ADD)
-        add_in_place(high01, HALF, 0, 2)
+            product_pass(z, third, 0, HALF, CHUNK, PACK)
         pick_and_add(2)
         pick(2, 0, last)
 
@@ -209,13 +211,13 @@ def tile_picked_posadd_none_p_kernel(
         pick_and_add(3)
         pick(3, 0, CHUNK)
         pick(3, CHUNK, CHUNK)
-        add_in_place(first23, 0, 2, 0)
-        nc.scalar.copy(lines(3).rearrange("p (g i t) -> p g t i", i=2, t=PACK), by_twos(hidden))
         pick(3, HALF, CHUNK)
-        add_as_words(middle23, CHUNK, 2, 1)
+        add_in_place(low23, 0, 2, PACK, 0)
+        nc.scalar.copy(slots(3, 2, PACK), by_twos(hidden))
+        add_as_words(low23, 0, 2, 1)
         weave(1)
-        second_layer(0, (4, 5), nc.scalar.copy, stores=2)
-        second_layer(3, (6, 7), nc.scalar.copy)
-        add_in_place(middle23, CHUNK, 2, 2)
-        second_layer(1, (1, 2), nc.vector.tensor_copy)
-        second_layer(2, (3, 4), nc.vector.tensor_copy)
+        second_layer(0, (5, 6), nc.scalar.copy, stores=2)
+        add_in_place(third, HALF, 0, PACK, 2)
+        second_layer(3, (7, 0), nc.vector.tensor_copy)
+        second_layer(1, (4, 1), nc.vector.tensor_copy)
+        second_layer(2, (3, 5), nc.vector.tensor_copy)

@@ -183,7 +183,10 @@ def tile_picked_posadd_none_p_kernel(
 
         out_rows = out.rearrange("(b p) s -> p b s", p=P)
 
-        def second_layer(c, tags, first_copy, stores=1):
+        banks_out = {}
+        result = sbuf("result", [P, 2 * S], F32)[:].rearrange("p (b s) -> p b s", b=2)
+
+        def second_product(c, order, tags):
             h_codes = sbuf(f"h_codes{c}", [P, CHUNK], U32)
             h_plane = sbuf(f"h_plane{c}", [P, CHUNK], U8)
             nc.vector.quantize_mx(
@@ -191,11 +194,10 @@ def tile_picked_posadd_none_p_kernel(
                 scales=h_plane[:],
                 in_=h_grouped[:, c * PACK * CHUNK : (c + 1) * PACK * CHUNK],
             )
-            result = sbuf(f"result{c}", [P, 2, CHUNK], F32)
-            for b, copy in enumerate((first_copy, nc.scalar.copy)):
-                bank = psum.tile([P, CHUNK], F32, name=f"second{c}{b}", tag=f"bank{tags[b]}")
+            for b, tag in zip(order, tags):
+                banks_out[c, b] = psum.tile([P, CHUNK], F32, name=f"second{c}{b}", tag=f"bank{tag}")
                 nc.tensor.matmul_mx(
-                    out=bank[:],
+                    out=banks_out[c, b][:],
                     lhsT=w2_codes[:, b * P : (b + 1) * P].bitcast(FP8X4),
                     lhsT_scale=w2_scale_rows[:, b * P : (b + 1) * P],
                     rhs=h_codes[:].bitcast(FP8X4),
@@ -203,10 +205,13 @@ def tile_picked_posadd_none_p_kernel(
                     start=True,
                     stop=True,
                 )
-                copy(result[:, b, :], bank[:])
-            for k in range(stores):
-                blocks = slice(k * 2 // stores, (k + 1) * 2 // stores)
-                nc.sync.dma_start(out_rows[:, blocks, c * CHUNK : (c + 1) * CHUNK], result[:, blocks, :])
+
+        def empty(c, b, copy):
+            copy(result[:, b, c * CHUNK : (c + 1) * CHUNK], banks_out[c, b][:])
+
+        def store(c0, c1, b0, b1):
+            cols = slice(c0 * CHUNK, c1 * CHUNK)
+            nc.sync.dma_start(out_rows[:, b0:b1, cols], result[:, b0:b1, cols])
 
         pick_and_add(3)
         pick(3, 0, CHUNK)
@@ -216,8 +221,16 @@ def tile_picked_posadd_none_p_kernel(
         nc.scalar.copy(slots(3, 2, PACK), by_twos(hidden))
         add_as_words(low23, 0, 2, 1)
         weave(1)
-        second_layer(0, (5, 6), nc.scalar.copy, stores=2)
+        second_product(0, (0, 1), (5, 6))
         add_in_place(third, HALF, 0, PACK, 2)
-        second_layer(3, (7, 0), nc.vector.tensor_copy)
-        second_layer(1, (4, 1), nc.vector.tensor_copy)
-        second_layer(2, (3, 5), nc.vector.tensor_copy)
+        for b in range(2):
+            empty(0, b, nc.scalar.copy)
+            store(0, 1, b, b + 1)
+        for c, tags in ((3, (7, 0)), (1, (4, 1)), (2, (3, 5))):
+            second_product(c, (0, 1), tags)
+        for c in (3, 1, 2):
+            empty(c, 0, nc.vector.tensor_copy)
+            empty(c, 1, nc.scalar.copy)
+        store(3, 4, 0, 2)
+        for b in range(2):
+            store(1, 3, b, b + 1)

@@ -92,7 +92,7 @@ def tile_picked_posadd_none_p_kernel(
         round_w1(1, nc.vector.tensor_copy, slice(0, 76))
         round_w1(1, nc.scalar.copy, slice(76, P))
         quantise_w1(1)
-        for first in (0, HALF):
+        for first in (HALF, 0):
             nc.vector.tensor_copy(x_codes[1][:, first : first + HALF], x_all[1][:].indirect(entries(first, HALF)))
         last = S - CHUNK
 
@@ -117,7 +117,7 @@ def tile_picked_posadd_none_p_kernel(
         last23 = product_bank("last23", CHUNK, "bank1")
         last01 = product_bank("last01", CHUNK, "bank2")
         low23 = product_bank("low23", HALF, "bank3")
-        early = [(low01, 0, 0, HALF), (last23, 2, last, CHUNK), (last01, 0, last, CHUNK), (low23, 2, 0, HALF)]
+        early = [(last01, 0, last, CHUNK), (last23, 2, last, CHUNK), (low01, 0, 0, HALF), (low23, 2, 0, HALF)]
         for z in range(PASSES):
             for unit in early:
                 product_pass(z, *unit)
@@ -169,13 +169,14 @@ def tile_picked_posadd_none_p_kernel(
 
         pick(0, 0, S)
         pick(1, 0, HALF)
-        nc.vector.tensor_copy(picked[:, 1, HALF:], window(1, HALF, HALF))
+        for first in (last, HALF):
+            nc.vector.tensor_copy(picked[:, 1, first : first + CHUNK], window(1, first, CHUNK))
         emptied = sbuf("emptied", [P, 2, CHUNK], F32, tag="pe_all1")
         nc.scalar.copy(emptied[:], last23[:])
+        add_in_place(last01, last, 0, 2, 3)
         add_in_place(low01, 0, 0, 2, 0)
         add_as_words(low01, 0, 0, 1)
-        add_in_place(last01, last, 0, 2, 3)
-        third = product_bank("third", CHUNK, "bank2", PACK)
+        third = product_bank("third", CHUNK, "bank0", PACK)
         for z in range(PASSES):
             product_pass(z, third, 0, HALF, CHUNK, PACK)
         pick_and_add(2)
@@ -226,7 +227,7 @@ def tile_picked_posadd_none_p_kernel(
         for b in range(2):
             empty(0, b, nc.scalar.copy)
             store(0, 1, b, b + 1)
-        for c, tags in ((3, (7, 0)), (1, (4, 1)), (2, (3, 5))):
+        for c, tags in ((3, (7, 2)), (1, (4, 1)), (2, (3, 5))):
             second_product(c, (0, 1), tags)
         for c in (3, 1, 2):
             empty(c, 0, nc.vector.tensor_copy)

from contextlib import ExitStack

import concourse.mybir as mybir

K, T, S, H, N = 1024, 1024, 512, 512, 256
FLOPS = 2 * K * H * S + 2 * H * N * S

F32 = mybir.dt.float32
BF16 = mybir.dt.bfloat16
I32 = mybir.dt.int32
U32 = mybir.dt.uint32
U16 = mybir.dt.uint16
U8 = mybir.dt.uint8
FP8X4 = mybir.dt.float8_e4m3fn_x4
ADD = mybir.AluOpType.add
COPY = mybir.ActivationFunctionType.Copy

P = 128
PACK = 4
PASSES = K // (P * PACK)
HALF = S // 2
CHUNK = 128
LIST_ROWS = 16


def tile_picked_posadd_none_p_kernel(
    tc, x_words, x_scales, w1, w2_words, w2_scales, pe, offs, out
):
    nc = tc.nc
    with ExitStack() as ctx:
        keep = ctx.enter_context(tc.tile_pool(name="keep", bufs=1))
        psum = ctx.enter_context(tc.psum_pool(name="psum", bufs=1))

        def sbuf(name, shape, dtype, tag=None):
            return keep.tile(shape, dtype, name=name, tag=tag or name, align_bytes=64)

        def entries(first, count):
            return offsets[:, first // LIST_ROWS : (first + count) // LIST_ROWS]

        offsets = keep.tile([P, S // LIST_ROWS], U16, name="offsets")
        x_scale_rows = sbuf("x_scale_rows", [P, T], U8)
        nc.vector.memset(x_scale_rows[:].bitcast(I32), 0)
        w2_scale_rows = sbuf("w2_scale_rows", [P, N], U8)
        nc.gpsimd.memset(w2_scale_rows[:].bitcast(I32), 0)

        pe_rows = pe.rearrange("(p t) c -> p t c", t=PACK)
        w1_rows = w1.rearrange("(z p j) c -> z p j c", p=P, j=PACK)
        x_all = [sbuf(f"x_all{z}", [P, T], U32) for z in range(PASSES)]
        w1_raw = [sbuf(f"w1_raw{z}", [P, PACK, H], F32) for z in range(PASSES)]
        pe_all = [sbuf(f"pe_all{t}", [P, T], F32) for t in range(PACK)]
        w2_codes = sbuf("w2_codes", [P, N], U32)

        def load_words(tile, words):
            nc.sync.dma_start(tile[:].bitcast(I32), words.rearrange("p n r -> p (n r)").bitcast(I32))

        nc.sync.dma_start(w1_raw[0][:], w1_rows[0])
        nc.sync.dma_start(offsets[:], offs)
        for q in range(4):
            nc.sync.dma_start(
                x_scale_rows[32 * q : 32 * q + 8, :].bitcast(I32),
                x_scales[:, 4 * q : 4 * q + 4, :].bitcast(I32),
            )
        load_words(x_all[0], x_words[0])
        nc.sync.dma_start(w1_raw[1][:], w1_rows[1])
        load_words(x_all[1], x_words[1])
        for t in range(PACK):
            nc.sync.dma_start(pe_all[t][:], pe_rows[:, t, :])
        load_words(w2_codes, w2_words[0])
        for q in range(4):
            nc.sync.dma_start(
                w2_scale_rows[32 * q : 32 * q + 4, :].bitcast(I32), w2_scales[0, 4 * q : 4 * q + 4, :].bitcast(I32)
            )

        x_planes = sbuf("x_planes", [P, S], U8)
        x_codes = [sbuf(f"x_codes{z}", [P, S], U32) for z in range(PASSES)]
        w1_grouped = [sbuf(f"w1_grouped{z}", [P, PACK * H], BF16) for z in range(PASSES)]
        w1_codes = {}
        w1_planes = [sbuf(f"w1_plane{z}", [P, H], U8) for z in range(PASSES)]

        def round_w1(z, copy, columns):
            dst = w1_grouped[z][:].rearrange("p (t m j) -> p m t j", t=PACK, j=PACK)[:, columns, :, :]
            copy(dst, w1_raw[z][:].rearrange("p j (m t) -> p m t j", t=PACK)[:, columns, :, :])

        def quantise_w1(z, tag=None):
            w1_codes[z] = sbuf(f"w1_codes{z}", [P, H], U32, tag=tag)
            nc.vector.quantize_mx(out=w1_codes[z][:].bitcast(FP8X4), scales=w1_planes[z][:], in_=w1_grouped[z][:])

        round_w1(0, nc.scalar.copy, slice(0, P))
        nc.vector.tensor_copy(x_planes[:], x_scale_rows[:].indirect(offsets[:]))
        nc.vector.tensor_copy(x_codes[0][:], x_all[0][:].indirect(offsets[:]))
        quantise_w1(0, tag="x_all0")
        round_w1(1, nc.vector.tensor_copy, slice(0, 76))
        round_w1(1, nc.scalar.copy, slice(76, P))
        quantise_w1(1)
        for first in (HALF, 0):
            nc.vector.tensor_copy(x_codes[1][:, first : first + HALF], x_all[1][:].indirect(entries(first, HALF)))
        last = S - CHUNK

        def product_bank(name, count, tag, phases=2):
            return psum.tile([P, phases, count], F32, name=name, tag=tag)

        def product_pass(z, bank, t0, first, count, phases=2):
            cols = slice(first, first + count)
            for slot in range(phases):
                rows = slice((t0 + slot) * P, (t0 + slot + 1) * P)
                nc.tensor.matmul_mx(
                    out=bank[:, slot, :],
                    lhsT=w1_codes[z][:, rows].bitcast(FP8X4),
                    lhsT_scale=w1_planes[z][:, rows],
                    rhs=x_codes[z][:, cols].bitcast(FP8X4),
                    rhs_scale=x_planes[4 * z : P, cols],
                    start=(z == 0 and slot == 0),
                    stop=(z == PASSES - 1 and slot == phases - 1),
                )

        low01 = product_bank("low01", HALF, "bank0")
        last23 = product_bank("last23", CHUNK, "bank1")
        last01 = product_bank("last01", CHUNK, "bank2")
        low23 = product_bank("low23", HALF, "bank3")
        early = [(last01, 0, last, CHUNK), (last23, 2, last, CHUNK), (low01, 0, 0, HALF), (low23, 2, 0, HALF)]
        for z in range(PASSES):
            for unit in early:
                product_pass(z, *unit)

        picked = sbuf("picked", [P, PACK * S], F32)[:].rearrange("p (t s) -> p t s", t=PACK)
        hidden = sbuf("hidden", [P, 2 * CHUNK], F32)[:].rearrange("p (t s) -> p t s", t=2)
        pairs = sbuf("pairs", [P, 2 * 2 * CHUNK], BF16)
        h_grouped = sbuf("h_grouped", [P, PACK * S], BF16)

        def window(t, first, count):
            return pe_all[t][:].indirect(entries(first, count))

        def pick(t, first, count):
            nc.scalar.activation(picked[:, t, first : first + count], window(t, first, count), COPY)

        def pick_and_add(t):
            nc.vector.tensor_tensor(hidden[:, t - 2, :], window(t, last, CHUNK), emptied[:, t - 2, :], ADD)

        def by_twos(planes):
            return planes.rearrange("p t (g i) -> p g t i", i=2)

        def lines(c):
            return h_grouped[:, c * PACK * CHUNK : (c + 1) * PACK * CHUNK]

        def add_planes(dst, bank, start, t0, t1, c):
            first = c * CHUNK
            nc.vector.tensor_tensor(
                dst,
                by_twos(bank[:, :, first - start : first - start + CHUNK]),
                by_twos(picked[:, t0:t1, first : first + CHUNK]),
                ADD,
            )

        def slots(c, t0, t1):
            return lines(c).rearrange("p (g i t) -> p g t i", i=2, t=PACK)[:, :, t0:t1, :]

        def add_in_place(bank, start, t0, t1, c):
            add_planes(slots(c, t0, t1), bank, start, t0, t1, c)

        def add_as_words(bank, start, t0, c):
            words = pairs[:, t0 * CHUNK : (t0 + 2) * CHUNK].rearrange("p (g i t) -> p g t i", i=2, t=2)
            add_planes(words, bank, start, t0, t0 + 2, c)

        def weave(c):
            nc.scalar.copy(
                lines(c).bitcast(U32).rearrange("p (s w) -> p s w", w=2),
                pairs[:].bitcast(U32).rearrange("p (w s) -> p s w", w=2),
            )

        pick(0, 0, S)
        pick(1, 0, HALF)
        for first in (last, HALF):
            nc.vector.tensor_copy(picked[:, 1, first : first + CHUNK], window(1, first, CHUNK))
        emptied = sbuf("emptied", [P, 2, CHUNK], F32, tag="pe_all1")
        nc.scalar.copy(emptied[:], last23[:])
        add_in_place(last01, last, 0, 2, 3)
        add_in_place(low01, 0, 0, 2, 0)
        add_as_words(low01, 0, 0, 1)
        third = product_bank("third", CHUNK, "bank0", PACK)
        for z in range(PASSES):
            product_pass(z, third, 0, HALF, CHUNK, PACK)
        pick_and_add(2)
        pick(2, 0, last)

        out_rows = out.rearrange("(b p) s -> p b s", p=P)

        banks_out = {}
        result = sbuf("result", [P, 2 * S], F32)[:].rearrange("p (b s) -> p b s", b=2)

        def second_product(c, order, tags):
            h_codes = sbuf(f"h_codes{c}", [P, CHUNK], U32)
            h_plane = sbuf(f"h_plane{c}", [P, CHUNK], U8)
            nc.vector.quantize_mx(
                out=h_codes[:].bitcast(FP8X4),
                scales=h_plane[:],
                in_=h_grouped[:, c * PACK * CHUNK : (c + 1) * PACK * CHUNK],
            )
            for b, tag in zip(order, tags):
                banks_out[c, b] = psum.tile([P, CHUNK], F32, name=f"second{c}{b}", tag=f"bank{tag}")
                nc.tensor.matmul_mx(
                    out=banks_out[c, b][:],
                    lhsT=w2_codes[:, b * P : (b + 1) * P].bitcast(FP8X4),
                    lhsT_scale=w2_scale_rows[:, b * P : (b + 1) * P],
                    rhs=h_codes[:].bitcast(FP8X4),
                    rhs_scale=h_plane[:],
                    start=True,
                    stop=True,
                )

        def empty(c, b, copy):
            copy(result[:, b, c * CHUNK : (c + 1) * CHUNK], banks_out[c, b][:])

        def store(c0, c1, b0, b1):
            cols = slice(c0 * CHUNK, c1 * CHUNK)
            nc.sync.dma_start(out_rows[:, b0:b1, cols], result[:, b0:b1, cols])

        pick_and_add(3)
        pick(3, 0, CHUNK)
        pick(3, CHUNK, CHUNK)
        pick(3, HALF, CHUNK)
        add_in_place(low23, 0, 2, PACK, 0)
        nc.scalar.copy(slots(3, 2, PACK), by_twos(hidden))
        add_as_words(low23, 0, 2, 1)
        weave(1)
        second_product(0, (0, 1), (5, 6))
        add_in_place(third, HALF, 0, PACK, 2)
        for b in range(2):
            empty(0, b, nc.scalar.copy)
            store(0, 1, b, b + 1)
        for c, tags in ((3, (7, 2)), (1, (4, 1)), (2, (3, 5))):
            second_product(c, (0, 1), tags)
        for c in (3, 1, 2):
            empty(c, 0, nc.vector.tensor_copy)
            empty(c, 1, nc.scalar.copy)
        store(3, 4, 0, 2)
        for b in range(2):
            store(1, 3, b, b + 1)
